import numpy as np
import ml_dtypes


def mxq(x, axis, fmt="e4m3"):
    dtype, down = {"e4m3": (ml_dtypes.float8_e4m3fn, 7), "e5m2": (ml_dtypes.float8_e5m2, 14)}[fmt]
    v = np.moveaxis(np.asarray(x, np.float32).astype(ml_dtypes.bfloat16).astype(np.float64), axis, -1)
    blocks = v.reshape(v.shape[:-1] + (-1, 32))
    amax = np.abs(blocks).max(-1, keepdims=True)
    byte = np.maximum(np.where(amax > 0, np.frexp(amax)[1] - 1 + 127, 0) - down, 1)
    scale = np.exp2(byte - 127.0)
    codes = (blocks / scale).astype(np.float32).astype(dtype).astype(np.float64)
    return np.moveaxis((codes * scale).reshape(v.shape), -1, axis)


WIDE = False


def mx_kscale(k):
    if not WIDE:
        return np.ones(k)
    levels = np.array([10, -10, 5, -5, 0])
    if k % 512:
        return np.exp2(np.random.permutation(np.resize(levels, k // 32))).repeat(32)
    a = np.empty((k // 512, 16))
    for p in range(k // 512):
        a[p, :8] = np.random.permutation(np.resize(levels, 8))
        for g in range(8):
            far = levels[np.abs(levels - a[p, g]) >= 10]
            a[p, g + 8] = far[np.random.randint(len(far))]
    return np.exp2(a.ravel()).repeat(32)


def f64(x):
    return np.asarray(x).astype(np.float64)


def striped(idx):
    return np.tile(idx.reshape(-1, 16).T, (8, 1)).astype(np.uint16)


def unstriped(offs):
    return offs[:16].T.reshape(-1).astype(np.int64)


def pack_weight(w):
    k, n = w.shape
    w = f64(np.asarray(w, np.float32).astype(ml_dtypes.bfloat16)).reshape(k // 32, 32, n)
    amax = np.abs(w).max(1)
    byte = np.clip(np.where(amax > 0, np.frexp(amax)[1] - 1 + 127 - 7, 1), 1, 254)
    scaled = (w * np.exp2(127.0 - byte)[:, None, :]).reshape(k, n).astype(np.float32)
    words = np.ascontiguousarray(scaled.reshape(k // 512, 128, 4, n).transpose(0, 1, 3, 2)).astype(ml_dtypes.float8_e4m3fn).view(np.uint8)
    return words, np.ascontiguousarray(byte.astype(np.uint8).reshape(k // 512, 16, n))


def unpack_weight(words, scales):
    g, p, n, _ = words.shape
    vals = np.ascontiguousarray(words).view(ml_dtypes.float8_e4m3fn).astype(np.float64) * np.repeat(np.exp2(scales.astype(np.float64) - 127.0), 8, axis=1)[..., None]
    return vals.transpose(0, 1, 3, 2).reshape(g * 512, n)


def planes(y):
    n, m = y.shape
    v = y.astype(np.float32).astype(ml_dtypes.bfloat16).astype(np.float64).reshape(n // 32, 32, m)
    top = np.abs(v).max(1)
    byte = np.clip(np.where(top > 0, np.frexp(top)[1] - 1 + 127 - 7, 1), 1, 254)
    codes = (v * np.exp2(127.0 - byte)[:, None, :]).reshape(n, m).astype(np.float32).astype(ml_dtypes.float8_e4m3fn).view(np.uint8)
    words = codes.reshape(n // 512, 128, 4, m).transpose(0, 1, 3, 2)
    return np.ascontiguousarray(words), np.ascontiguousarray(byte.astype(np.uint8).reshape(n // 512, 16, m))


def relu(v):
    return np.maximum(v, 0.0)


K, T, S, H, N, V = 1024, 4096, 1024, 512, 512, 512
P = 2 ** 7


def setup_inputs():
    n = np.random.standard_normal
    s = mx_kscale(K)[:, None]
    u = mx_kscale(H)
    perm = np.random.permutation(S)
    packed_xT = pack_weight(n((K, T)) * s)
    return {
        "x_words": packed_xT[0],
        "x_scales": packed_xT[1],
        "w1": (n((K, H)) / np.sqrt(K) / s * u).astype(np.float32),
        "w2": (n((H, N)) / np.sqrt(H) / u[:, None]).astype(np.float32),
        "gate": (np.tile(np.random.uniform(0.2, 1.0, V), (P, 1))).astype(np.float32),
        "back": (np.tile(np.random.uniform(0.5, 1.5, V), (P, 1))).astype(np.float32),
        "offs": striped(np.random.permutation(T)[:S]),
        "ka": striped(perm[:V]),
        "kb": striped(perm[V:]),
    }


def reference(x_words, x_scales, w1, w2, gate, back, offs, ka, kb):
    xq = unpack_weight(x_words, x_scales)[:, unstriped(offs)]
    h = relu(mxq(f64(w1), 0, "e4m3").T @ xq)
    z = h[:, unstriped(ka)] + h[:, unstriped(kb)] * f64(gate)[:1]
    y = mxq(f64(w2), 0, "e4m3").T @ mxq(z, 0, "e4m3")
    yb = y * f64(back)[:1]
    out = np.zeros((H, S))
    out[:, unstriped(ka)] = y
    res = out.copy()
    res[:, unstriped(kb)] = yb
    out_0 = res
    return (out_0,) + planes(out_0)

@@ -1,0 +1,265 @@
+from contextlib import ExitStack
+
+import concourse.mybir as mybir
+
+K, T, S, H, N, V = 1024, 4096, 1024, 512, 512, 512
+FLOPS = 2 * K * H * S + 2 * H * N * V
+
+F32 = mybir.dt.float32
+BF16 = mybir.dt.bfloat16
+I32 = mybir.dt.int32
+U32 = mybir.dt.uint32
+U16 = mybir.dt.uint16
+U8 = mybir.dt.uint8
+FP8X4 = mybir.dt.float8_e4m3fn_x4
+MULT = mybir.AluOpType.mult
+ADD = mybir.AluOpType.add
+MAX = mybir.AluOpType.max
+RELU = mybir.ActivationFunctionType.Relu
+
+P = 128
+PACK = 4
+K_PASS = P * PACK
+BANK = 512
+CHUNK = 256
+LIST_ROWS = 16
+
+
+def tile_picked_zunm_relu_po_kernel(
+    tc, x_words, x_scales, w1, w2, gate, back, offs, ka, kb, out_0, out_1, out_2
+):
+    nc = tc.nc
+    passes = K // K_PASS
+    chunks = V // CHUNK
+
+    with ExitStack() as ctx:
+        keep = ctx.enter_context(tc.tile_pool(name="keep", bufs=1))
+        psum = ctx.enter_context(tc.psum_pool(name="psum", bufs=8))
+
+        def entries(list_tile, start, count):
+            return list_tile[:, start // LIST_ROWS : (start + count) // LIST_ROWS]
+
+        offs_sb = keep.tile([P, S // LIST_ROWS], U16, name="offs_sb")
+        ka_sb = keep.tile([P, V // LIST_ROWS], U16, name="ka_sb")
+        kb_sb = keep.tile([P, V // LIST_ROWS], U16, name="kb_sb")
+        table = [keep.tile([P, T], U32, name="table%d" % o) for o in range(passes)]
+        table_scales = keep.tile([P, T], U8, name="table_scales", tag="scales_then_codes", align_bytes=64)
+        w1_first = keep.tile([P, PACK, H], F32, name="w1_first")
+        w1_second = [keep.tile([P, PACK, H // 2], F32, name="w1_second%d" % c) for c in range(2)]
+        w2_raw = keep.tile([P, PACK, N], F32, name="w2_raw")
+        gate_sb = keep.tile([P, V], F32, name="gate_sb")
+        back_sb = keep.tile([P, V], F32, name="back_sb")
+
+        def load_table(o):
+            nc.sync.dma_start(
+                out=table[o][:].bitcast(I32),
+                in_=x_words[o].rearrange("p n t -> p (n t)").bitcast(I32),
+            )
+
+        w1_rows = w1.rearrange("(o p j) c -> o p j c", o=passes, j=PACK)
+        nc.vector.memset(table_scales[:].bitcast(I32), 0)
+        nc.sync.dma_start(offs_sb[:], offs)
+        load_table(0)
+        for q in range(4):
+            nc.gpsimd.dma_start(
+                out=table_scales[32 * q : 32 * q + 4 * passes, :].bitcast(I32),
+                in_=x_scales[:, 4 * q : 4 * q + 4, :].bitcast(I32),
+            )
+        nc.sync.dma_start(out=w1_first[:], in_=w1_rows[0])
+        load_table(1)
+        nc.sync.dma_start(kb_sb[:], kb)
+        nc.sync.dma_start(ka_sb[:], ka)
+        for c in range(2):
+            nc.sync.dma_start(out=w1_second[c][:], in_=w1_rows[1][:, :, c * (H // 2) : (c + 1) * (H // 2)])
+        nc.sync.dma_start(out=gate_sb[:], in_=gate)
+        nc.sync.dma_start(out=w2_raw[:], in_=w2.rearrange("(p j) c -> p j c", j=PACK))
+        nc.sync.dma_start(out=back_sb[:], in_=back)
+
+        x_codes = [keep.tile([P, S], U32, name="x_codes0", align_bytes=64)]
+        x_planes = keep.tile([P, S], U8, name="x_planes", align_bytes=64)
+        nc.vector.tensor_copy(x_codes[0][:], table[0][:].indirect(offs_sb[:]))
+        nc.vector.tensor_copy(x_planes[:], table_scales[:].indirect(offs_sb[:]))
+
+        def deal(copy, grouped, raw, m0, m_count, raw_m0):
+            copy(
+                grouped[:, :, m0 : m0 + m_count, :],
+                raw[:, :, PACK * raw_m0 : PACK * (raw_m0 + m_count)].rearrange("p j (m t) -> p t m j", t=PACK),
+            )
+
+        w1_grouped = [keep.tile([P, PACK, P, PACK], BF16, name="w1_grouped%d" % o, align_bytes=64) for o in range(passes)]
+        w1_codes = [keep.tile([P, H], U32, name="w1_codes%d" % o, align_bytes=64) for o in range(passes)]
+        w1_planes = [keep.tile([P, H], U8, name="w1_planes%d" % o, align_bytes=64) for o in range(passes)]
+
+        deal(nc.scalar.copy, w1_grouped[0], w1_first, 0, P, 0)
+        nc.vector.quantize_mx(
+            out=w1_codes[0][:].bitcast(FP8X4),
+            scales=w1_planes[0][:],
+            in_=w1_grouped[0][:].rearrange("p t m j -> p (t m j)"),
+        )
+        halves = S // BANK
+        acc = [[psum.tile([P, BANK], F32, name="acc", tag="bank") for half in range(halves)] for t in range(PACK)]
+
+        def first_product(o, t, half):
+            cols = slice(P * t, P * (t + 1))
+            tokens = slice(BANK * half, BANK * (half + 1))
+            nc.tensor.matmul_mx(
+                out=acc[t][half][:],
+                lhsT=w1_codes[o][:, cols].bitcast(FP8X4),
+                lhsT_scale=w1_planes[o][:, cols],
+                rhs=x_codes[o][:, tokens].bitcast(FP8X4),
+                rhs_scale=x_planes[4 * o : P, tokens],
+                start=(o == 0),
+                stop=(o == passes - 1),
+            )
+
+        for t in range(PACK):
+            for half in range(halves):
+                first_product(0, t, half)
+
+        x_codes.append(keep.tile([P, S], U32, name="x_codes1", tag="scales_then_codes", align_bytes=64))
+        nc.vector.tensor_copy(x_codes[1][:], table[1][:].indirect(offs_sb[:]))
+        deal(nc.scalar.copy, w1_grouped[1], w1_second[0], 0, 64, 0)
+        deal(nc.vector.tensor_copy, w1_grouped[1], w1_second[1], 64, 40, 0)
+        deal(nc.scalar.copy, w1_grouped[1], w1_second[1], 104, 24, 40)
+
+        h = [keep.tile([P, S], F32, name="h%d" % t) for t in range(PACK)]
+        for t in range(PACK):
+            cols = slice(P * t, P * (t + 1))
+            nc.vector.quantize_mx(
+                out=w1_codes[1][:, cols].bitcast(FP8X4),
+                scales=w1_planes[1][:, cols],
+                in_=w1_grouped[1][:, t].rearrange("p m j -> p (m j)"),
+            )
+        for t in range(PACK):
+            for half in range(halves):
+                first_product(1, t, half)
+                tokens = slice(BANK * half, BANK * (half + 1))
+                if t == 0 and half == 0:
+                    nc.vector.tensor_scalar(h[t][:, tokens], acc[t][half][:], 0.0, None, MAX)
+                else:
+                    nc.scalar.activation(h[t][:, tokens], acc[t][half][:], RELU)
+
+        w2_grouped = keep.tile([P, PACK, P, PACK], BF16, name="w2_grouped", align_bytes=64)
+        w2_codes = keep.tile([P, N], U32, name="w2_codes", align_bytes=64)
+        w2_planes = keep.tile([P, N], U8, name="w2_planes", align_bytes=64)
+        for c in range(2):
+            deal(nc.scalar.copy, w2_grouped, w2_raw, 64 * c, 64, 64 * c)
+
+        z_grouped = [keep.tile([P, CHUNK, PACK], BF16, name="z_grouped%d" % c, align_bytes=64) for c in range(chunks)]
+        z_codes = [keep.tile([P, CHUNK], U32, name="z_codes%d" % c, align_bytes=64) for c in range(chunks)]
+        z_planes = [keep.tile([P, CHUNK], U8, name="z_planes%d" % c, align_bytes=64) for c in range(chunks)]
+        z = [keep.tile([P, PACK, CHUNK], F32, name="z%d" % c) for c in range(chunks)]
+        gated = [keep.tile([P, PACK, CHUNK], F32, name="gated%d" % c) for c in range(chunks)]
+        order = (2, 0, 1, 3)
+        y = {}
+        banks = {}
+
+        def merge(c, tiles):
+            pairs = slice(CHUNK * c, CHUNK * (c + 1))
+            for t in tiles:
+                nc.vector.tensor_tensor(
+                    gated[c][:, t, :], h[t][:].indirect(entries(kb_sb, CHUNK * c, CHUNK)), gate_sb[:, pairs], MULT
+                )
+            for t in tiles:
+                nc.vector.tensor_tensor(
+                    z[c][:, t, :], h[t][:].indirect(entries(ka_sb, CHUNK * c, CHUNK)), gated[c][:, t, :], ADD
+                )
+
+        def regroup(c):
+            nc.scalar.copy(
+                z_grouped[c][:].rearrange("p (a i) t -> p a t i", i=4),
+                z[c][:].rearrange("p t (a i) -> p a t i", i=4),
+            )
+
+        def second_product(c):
+            nc.vector.quantize_mx(
+                out=z_codes[c][:].bitcast(FP8X4),
+                scales=z_planes[c][:],
+                in_=z_grouped[c][:].rearrange("p v t -> p (v t)"),
+            )
+            for t in order:
+                cols = slice(P * t, P * (t + 1))
+                bank = psum.tile([P, BANK], F32, name="bank", tag="bank")
+                nc.tensor.matmul_mx(
+                    out=bank[:, 0:CHUNK],
+                    lhsT=w2_codes[:, cols].bitcast(FP8X4),
+                    lhsT_scale=w2_planes[:, cols],
+                    rhs=z_codes[c][:].bitcast(FP8X4),
+                    rhs_scale=z_planes[c][:],
+                    start=True,
+                    stop=True,
+                )
+                banks[c, t] = bank
+
+        def unload(c, t, tag):
+            y[c, t] = keep.tile([P, CHUNK], F32, name="y", tag=tag)
+            nc.scalar.copy(y[c, t][:], banks[c, t][:, 0:CHUNK])
+
+        merge(0, (0, 1))
+        merge(0, (2, 3))
+        regroup(0)
+        nc.vector.quantize_mx(
+            out=w2_codes[:].bitcast(FP8X4),
+            scales=w2_planes[:],
+            in_=w2_grouped[:].rearrange("p t m j -> p (t m j)"),
+        )
+        merge(1, (0, 1))
+        second_product(0)
+        for t in order:
+            unload(0, t, "y0_%d" % t)
+        merge(1, (2, 3))
+        regroup(1)
+
+        window = [keep.tile([P, S], F32, name="window%d" % t) for t in range(PACK)]
+        out_rows = out_0.rearrange("(p t) c -> p t c", t=PACK)
+        out_grouped = keep.tile([P, S, PACK], BF16, name="out_grouped", align_bytes=64)
+
+        def scatter(c, t):
+            pairs = slice(CHUNK * c, CHUNK * (c + 1))
+            nc.vector.tensor_copy(window[t][:].indirect(entries(ka_sb, CHUNK * c, CHUNK)), y[c, t][:])
+            nc.vector.tensor_tensor(
+                window[t][:].indirect(entries(kb_sb, CHUNK * c, CHUNK)), y[c, t][:], back_sb[:, pairs], MULT
+            )
+
+        scatter(0, order[0])
+        second_product(1)
+        for t in order[:-1]:
+            unload(1, t, "y1_%d" % t)
+        scatter(0, order[1])
+        for n, t in enumerate(order):
+            if n >= 2:
+                scatter(0, t)
+            scatter(1, t)
+            nc.sync.dma_start(out=out_rows[:, t, :], in_=window[t][:])
+            if n == 1:
+                unload(1, order[-1], "y1_%d" % t)
+            if n < PACK - 1:
+                nc.scalar.copy(out_grouped[:, :, t], window[t][:])
+
+        last = order[-1]
+        quarter = S // 4
+        out_codes = keep.tile([P, S], U32, name="out_codes", align_bytes=64)
+        out_planes = keep.tile([P, S], U8, name="out_planes", align_bytes=64)
+        for j in range(4):
+            cols = slice(quarter * j, quarter * (j + 1))
+            if j < 2:
+                nc.vector.tensor_copy(out_grouped[:, cols, last], window[last][:, cols])
+            else:
+                nc.scalar.copy(out_grouped[:, cols, last], window[last][:, cols])
+        words_out = out_1[0].rearrange("p n t -> p (n t)").bitcast(I32)
+        for j in range(4):
+            cols = slice(quarter * j, quarter * (j + 1))
+            nc.vector.quantize_mx(
+                out=out_codes[:, cols].bitcast(FP8X4),
+                scales=out_planes[:, cols],
+                in_=out_grouped[:, cols, :].rearrange("p c t -> p (c t)"),
+            )
+            if j % 2 == 1:
+                both = slice(quarter * (j - 1), quarter * (j + 1))
+                nc.sync.dma_start(out=words_out[:, both], in_=out_codes[:, both].bitcast(I32))
+        for q in range(4):
+            queue = nc.scalar if q % 2 else nc.sync
+            queue.dma_start(
+                out=out_2[0, 4 * q : 4 * q + 4, :].bitcast(I32),
+                in_=out_planes[32 * q : 32 * q + 4, :].bitcast(I32),
+            )

@@ -1,6 +1,7 @@
 from contextlib import ExitStack
 
 import concourse.mybir as mybir
+from concourse.masks import make_identity
 
 K, T, S, H, N, V = 1024, 4096, 1024, 512, 512, 512
 FLOPS = 2 * K * H * S + 2 * H * N * V
@@ -13,7 +14,6 @@ U16 = mybir.dt.uint16
 U8 = mybir.dt.uint8
 FP8X4 = mybir.dt.float8_e4m3fn_x4
 MULT = mybir.AluOpType.mult
-ADD = mybir.AluOpType.add
 MAX = mybir.AluOpType.max
 RELU = mybir.ActivationFunctionType.Relu
 
@@ -21,57 +21,74 @@ P = 128
 PACK = 4
 K_PASS = P * PACK
 BANK = 512
-CHUNK = 256
 LIST_ROWS = 16
+PASSES = K // K_PASS
+EARLY = 128
+LATE = V - EARLY
 
 
 def tile_picked_zunm_relu_po_kernel(
     tc, x_words, x_scales, w1, w2, gate, back, offs, ka, kb, out_0, out_1, out_2
 ):
     nc = tc.nc
-    passes = K // K_PASS
-    chunks = V // CHUNK
 
     with ExitStack() as ctx:
         keep = ctx.enter_context(tc.tile_pool(name="keep", bufs=1))
-        psum = ctx.enter_context(tc.psum_pool(name="psum", bufs=8))
+        psum = ctx.enter_context(tc.psum_pool(name="psum", bufs=1))
 
         def entries(list_tile, start, count):
             return list_tile[:, start // LIST_ROWS : (start + count) // LIST_ROWS]
 
+        def quantize(codes, planes, grouped):
+            nc.vector.quantize_mx(out=codes.bitcast(FP8X4), scales=planes, in_=grouped)
+
+        def interleave(copy, grouped, raw):
+            copy(grouped.rearrange("p (a i) j -> p a j i", i=4), raw.rearrange("p j (a i) -> p a j i", i=4))
+
         offs_sb = keep.tile([P, S // LIST_ROWS], U16, name="offs_sb")
         ka_sb = keep.tile([P, V // LIST_ROWS], U16, name="ka_sb")
         kb_sb = keep.tile([P, V // LIST_ROWS], U16, name="kb_sb")
-        table = [keep.tile([P, T], U32, name="table%d" % o) for o in range(passes)]
+        table = [keep.tile([P, T], U32, name="table%d" % o) for o in range(PASSES)]
         table_scales = keep.tile([P, T], U8, name="table_scales", tag="scales_then_codes", align_bytes=64)
-        w1_first = keep.tile([P, PACK, H], F32, name="w1_first")
-        w1_second = [keep.tile([P, PACK, H // 2], F32, name="w1_second%d" % c) for c in range(2)]
+        w1_parts = ((0, P), (P, P), (2 * P, 2 * P))
+        w1_raw = [
+            [keep.tile([P, PACK, width], F32, name="w1_raw%d_%d" % (n, o)) for o in range(PASSES)]
+            for n, (first, width) in enumerate(w1_parts)
+        ]
         w2_raw = keep.tile([P, PACK, N], F32, name="w2_raw")
         gate_sb = keep.tile([P, V], F32, name="gate_sb")
         back_sb = keep.tile([P, V], F32, name="back_sb")
+        identity = keep.tile([P, P], F32, name="identity")
 
-        def load_table(o):
-            nc.sync.dma_start(
-                out=table[o][:].bitcast(I32),
-                in_=x_words[o].rearrange("p n t -> p (n t)").bitcast(I32),
-            )
+        def load_table(o, pieces):
+            words = x_words[o].rearrange("p n t -> p (n t)").bitcast(I32)
+            for c in range(pieces):
+                cols = slice(c * T // pieces, (c + 1) * T // pieces)
+                nc.sync.dma_start(out=table[o][:, cols].bitcast(I32), in_=words[:, cols])
 
-        w1_rows = w1.rearrange("(o p j) c -> o p j c", o=passes, j=PACK)
+        w1_rows = w1.rearrange("(o p j) c -> o p j c", o=PASSES, j=PACK)
+
+        def load_w1(n):
+            first, width = w1_parts[n]
+            for o in range(PASSES):
+                nc.sync.dma_start(out=w1_raw[n][o][:], in_=w1_rows[o][:, :, first : first + width])
+
         nc.vector.memset(table_scales[:].bitcast(I32), 0)
+        make_identity(nc, identity[:])
         nc.sync.dma_start(offs_sb[:], offs)
-        load_table(0)
-        for q in range(4):
-            nc.gpsimd.dma_start(
-                out=table_scales[32 * q : 32 * q + 4 * passes, :].bitcast(I32),
-                in_=x_scales[:, 4 * q : 4 * q + 4, :].bitcast(I32),
-            )
-        nc.sync.dma_start(out=w1_first[:], in_=w1_rows[0])
-        load_table(1)
         nc.sync.dma_start(kb_sb[:], kb)
         nc.sync.dma_start(ka_sb[:], ka)
-        for c in range(2):
-            nc.sync.dma_start(out=w1_second[c][:], in_=w1_rows[1][:, :, c * (H // 2) : (c + 1) * (H // 2)])
+        load_table(0, 4)
+        for q in range(4):
+            nc.sync.dma_start(
+                out=table_scales[32 * q : 32 * q + 4 * PASSES, :].bitcast(I32),
+                in_=x_scales[:, 4 * q : 4 * q + 4, :].bitcast(I32),
+            )
+        load_w1(0)
+        load_table(1, 1)
+        load_w1(1)
         nc.sync.dma_start(out=gate_sb[:], in_=gate)
+        load_w1(2)
         nc.sync.dma_start(out=w2_raw[:], in_=w2.rearrange("(p j) c -> p j c", j=PACK))
         nc.sync.dma_start(out=back_sb[:], in_=back)
 
@@ -80,180 +97,235 @@ def tile_picked_zunm_relu_po_kernel(
         nc.vector.tensor_copy(x_codes[0][:], table[0][:].indirect(offs_sb[:]))
         nc.vector.tensor_copy(x_planes[:], table_scales[:].indirect(offs_sb[:]))
 
-        def deal(copy, grouped, raw, m0, m_count, raw_m0):
-            copy(
-                grouped[:, :, m0 : m0 + m_count, :],
-                raw[:, :, PACK * raw_m0 : PACK * (raw_m0 + m_count)].rearrange("p j (m t) -> p t m j", t=PACK),
+        w1_codes = [keep.tile([P, PASSES, P], U32, name="w1_codes%d" % t, align_bytes=64) for t in range(PACK)]
+        w1_planes = [keep.tile([P, PASSES, P], U8, name="w1_planes%d" % t, align_bytes=64) for t in range(PACK)]
+        h = {}
+        h_slots = ("w1_raw1_1", "w1_raw2_1", "h2", "h3")
+        halves = S // BANK
+        acc = {}
+
+        def prepare_w1(t):
+            n = min(t, 2)
+            first = P * t - w1_parts[n][0]
+            grouped = keep.tile([P, PASSES, P, PACK], BF16, name="w1_grouped%d" % t, align_bytes=64)
+            for o in range(PASSES):
+                interleave(nc.scalar.copy, grouped[:, o], w1_raw[n][o][:, :, first : first + P])
+            quantize(
+                w1_codes[t][:].rearrange("p o m -> p (o m)"),
+                w1_planes[t][:].rearrange("p o m -> p (o m)"),
+                grouped[:].rearrange("p o m j -> p (o m j)"),
             )
 
-        w1_grouped = [keep.tile([P, PACK, P, PACK], BF16, name="w1_grouped%d" % o, align_bytes=64) for o in range(passes)]
-        w1_codes = [keep.tile([P, H], U32, name="w1_codes%d" % o, align_bytes=64) for o in range(passes)]
-        w1_planes = [keep.tile([P, H], U8, name="w1_planes%d" % o, align_bytes=64) for o in range(passes)]
-
-        deal(nc.scalar.copy, w1_grouped[0], w1_first, 0, P, 0)
-        nc.vector.quantize_mx(
-            out=w1_codes[0][:].bitcast(FP8X4),
-            scales=w1_planes[0][:],
-            in_=w1_grouped[0][:].rearrange("p t m j -> p (t m j)"),
-        )
-        halves = S // BANK
-        acc = [[psum.tile([P, BANK], F32, name="acc", tag="bank") for half in range(halves)] for t in range(PACK)]
-
         def first_product(o, t, half):
-            cols = slice(P * t, P * (t + 1))
             tokens = slice(BANK * half, BANK * (half + 1))
+            if o == 0:
+                acc[t, half] = psum.tile([P, BANK], F32, name="acc", tag="bank%d" % (halves * t + half))
             nc.tensor.matmul_mx(
-                out=acc[t][half][:],
-                lhsT=w1_codes[o][:, cols].bitcast(FP8X4),
-                lhsT_scale=w1_planes[o][:, cols],
+                out=acc[t, half][:],
+                lhsT=w1_codes[t][:, o, :].bitcast(FP8X4),
+                lhsT_scale=w1_planes[t][:, o, :],
                 rhs=x_codes[o][:, tokens].bitcast(FP8X4),
                 rhs_scale=x_planes[4 * o : P, tokens],
                 start=(o == 0),
-                stop=(o == passes - 1),
+                stop=(o == PASSES - 1),
             )
 
-        for t in range(PACK):
-            for half in range(halves):
-                first_product(0, t, half)
+        def relu(t, half):
+            tokens = slice(BANK * half, BANK * (half + 1))
+            if half == 0:
+                h[t] = keep.tile([P, S], F32, name="h", tag=h_slots[t])
+            if (t, half) == (0, halves - 1):
+                nc.vector.tensor_scalar(h[t][:, tokens], acc[t, half][:], 0.0, None, MAX)
+            else:
+                nc.scalar.activation(h[t][:, tokens], acc[t, half][:], RELU)
 
+        prepare_w1(0)
+        for half in range(halves):
+            first_product(0, 0, half)
         x_codes.append(keep.tile([P, S], U32, name="x_codes1", tag="scales_then_codes", align_bytes=64))
-        nc.vector.tensor_copy(x_codes[1][:], table[1][:].indirect(offs_sb[:]))
-        deal(nc.scalar.copy, w1_grouped[1], w1_second[0], 0, 64, 0)
-        deal(nc.vector.tensor_copy, w1_grouped[1], w1_second[1], 64, 40, 0)
-        deal(nc.scalar.copy, w1_grouped[1], w1_second[1], 104, 24, 40)
+        for half in range(halves):
+            tokens = slice(BANK * half, BANK * (half + 1))
+            nc.vector.tensor_copy(x_codes[1][:, tokens], table[1][:].indirect(entries(offs_sb, BANK * half, BANK)))
+            first_product(1, 0, half)
+        prepare_w1(1)
+        for half in range(halves):
+            relu(0, half)
 
-        h = [keep.tile([P, S], F32, name="h%d" % t) for t in range(PACK)]
-        for t in range(PACK):
-            cols = slice(P * t, P * (t + 1))
-            nc.vector.quantize_mx(
-                out=w1_codes[1][:, cols].bitcast(FP8X4),
-                scales=w1_planes[1][:, cols],
-                in_=w1_grouped[1][:, t].rearrange("p m j -> p (m j)"),
-            )
-        for t in range(PACK):
+        def hidden_rows(t):
             for half in range(halves):
-                first_product(1, t, half)
-                tokens = slice(BANK * half, BANK * (half + 1))
-                if t == 0 and half == 0:
-                    nc.vector.tensor_scalar(h[t][:, tokens], acc[t][half][:], 0.0, None, MAX)
-                else:
-                    nc.scalar.activation(h[t][:, tokens], acc[t][half][:], RELU)
+                for o in range(PASSES):
+                    first_product(o, t, half)
+                relu(t, half)
 
-        w2_grouped = keep.tile([P, PACK, P, PACK], BF16, name="w2_grouped", align_bytes=64)
-        w2_codes = keep.tile([P, N], U32, name="w2_codes", align_bytes=64)
-        w2_planes = keep.tile([P, N], U8, name="w2_planes", align_bytes=64)
-        for c in range(2):
-            deal(nc.scalar.copy, w2_grouped, w2_raw, 64 * c, 64, 64 * c)
+        z_turned = {}
+        picked = {}
 
-        z_grouped = [keep.tile([P, CHUNK, PACK], BF16, name="z_grouped%d" % c, align_bytes=64) for c in range(chunks)]
-        z_codes = [keep.tile([P, CHUNK], U32, name="z_codes%d" % c, align_bytes=64) for c in range(chunks)]
-        z_planes = [keep.tile([P, CHUNK], U8, name="z_planes%d" % c, align_bytes=64) for c in range(chunks)]
-        z = [keep.tile([P, PACK, CHUNK], F32, name="z%d" % c) for c in range(chunks)]
-        gated = [keep.tile([P, PACK, CHUNK], F32, name="gated%d" % c) for c in range(chunks)]
-        order = (2, 0, 1, 3)
-        y = {}
-        banks = {}
+        def pick(t, start, count, tags):
+            first = keep.tile([P, count], F32, name="first", tag=tags[0], align_bytes=64)
+            second = keep.tile([P, count], F32, name="second", tag=tags[1], align_bytes=64)
+            nc.vector.tensor_copy(first[:], h[t][:].indirect(entries(ka_sb, start, count)))
+            nc.vector.tensor_tensor(
+                second[:], h[t][:].indirect(entries(kb_sb, start, count)), gate_sb[:, start : start + count], MULT
+            )
+            for b in range(count // P):
+                cols = slice(P * b, P * (b + 1))
+                picked[t, start // P + b] = (first[:, cols], second[:, cols])
 
-        def merge(c, tiles):
-            pairs = slice(CHUNK * c, CHUNK * (c + 1))
+        def add_turned(block, tiles):
+            if block not in z_turned:
+                z_turned[block] = psum.tile([P, H], F32, name="z_turned", tag="bank%d" % (6, 7, 4, 6)[block])
             for t in tiles:
-                nc.vector.tensor_tensor(
-                    gated[c][:, t, :], h[t][:].indirect(entries(kb_sb, CHUNK * c, CHUNK)), gate_sb[:, pairs], MULT
-                )
-            for t in tiles:
-                nc.vector.tensor_tensor(
-                    z[c][:, t, :], h[t][:].indirect(entries(ka_sb, CHUNK * c, CHUNK)), gated[c][:, t, :], ADD
-                )
+                first, second = picked[t, block]
+                target = z_turned[block][:, P * t : P * (t + 1)]
+                nc.tensor.matmul(target, first, identity[:], start=True, stop=False, is_transpose=True)
+                nc.tensor.matmul(target, second, identity[:], start=False, stop=True, is_transpose=True)
 
-        def regroup(c):
+        def regroup(first_block, count, name, bank):
+            words = psum.tile([P, count, 2, P], F32, name="words", tag=bank)
+            grouped = keep.tile([P, count * P, PACK], BF16, name="grouped", tag=name + "_grouped", align_bytes=64)
+            for b in range(count):
+                rounded = keep.tile([P, 2, P, 2], BF16, name="rounded", tag=name + "_rounded%d" % b, align_bytes=64)
+                nc.scalar.copy(rounded[:], z_turned[first_block + b][:].rearrange("v (p u e) -> v u p e", u=2, e=2))
+                for u in range(2):
+                    nc.tensor.transpose(words[:, b, u, :], rounded[:, u].rearrange("v p e -> v (p e)").bitcast(F32), identity[:])
             nc.scalar.copy(
-                z_grouped[c][:].rearrange("p (a i) t -> p a t i", i=4),
-                z[c][:].rearrange("p t (a i) -> p a t i", i=4),
+                grouped[:].rearrange("p v t -> p (v t)").bitcast(F32).rearrange("p (b v u) -> p b v u", b=count, u=2),
+                words[:].rearrange("p b u v -> p b v u"),
+            )
+            codes = keep.tile([P, count * P], U32, name="codes", tag=name + "_codes", align_bytes=64)
+            planes = keep.tile([P, count * P], U8, name="planes", tag=name + "_planes", align_bytes=64)
+            quantize(codes[:], planes[:], grouped[:].rearrange("p v t -> p (v t)"))
+            return codes, planes
+
+        order = (0, 2, 3, 1)
+        w2_codes = {}
+        w2_planes = {}
+
+        def prepare_w2(odd):
+            grouped = keep.tile([P, 2, P, PACK], BF16, name="w2_grouped%d" % odd, align_bytes=64)
+            codes = keep.tile([P, 2, P], U32, name="w2_codes%d" % odd, align_bytes=64)
+            planes = keep.tile([P, 2, P], U8, name="w2_planes%d" % odd, align_bytes=64)
+            nc.scalar.copy(
+                grouped[:].rearrange("p s m j -> p m j s"),
+                w2_raw[:].rearrange("p j (m s e) -> p e m j s", s=2, e=2)[:, odd],
+            )
+            quantize(
+                codes[:].rearrange("p s m -> p (s m)"),
+                planes[:].rearrange("p s m -> p (s m)"),
+                grouped[:].rearrange("p s m j -> p (s m j)"),
+            )
+            for s in range(2):
+                w2_codes[2 * s + odd] = codes[:, s, :]
+                w2_planes[2 * s + odd] = planes[:, s, :]
+
+        def second_product(target, t, operand):
+            codes, planes = operand
+            nc.tensor.matmul_mx(
+                out=target,
+                lhsT=w2_codes[t].bitcast(FP8X4),
+                lhsT_scale=w2_planes[t],
+                rhs=codes[:].bitcast(FP8X4),
+                rhs_scale=planes[:],
+                start=True,
+                stop=True,
             )
 
-        def second_product(c):
-            nc.vector.quantize_mx(
-                out=z_codes[c][:].bitcast(FP8X4),
-                scales=z_planes[c][:],
-                in_=z_grouped[c][:].rearrange("p v t -> p (v t)"),
-            )
-            for t in order:
-                cols = slice(P * t, P * (t + 1))
-                bank = psum.tile([P, BANK], F32, name="bank", tag="bank")
-                nc.tensor.matmul_mx(
-                    out=bank[:, 0:CHUNK],
-                    lhsT=w2_codes[:, cols].bitcast(FP8X4),
-                    lhsT_scale=w2_planes[:, cols],
-                    rhs=z_codes[c][:].bitcast(FP8X4),
-                    rhs_scale=z_planes[c][:],
-                    start=True,
-                    stop=True,
-                )
-                banks[c, t] = bank
+        y = {}
 
-        def unload(c, t, tag):
-            y[c, t] = keep.tile([P, CHUNK], F32, name="y", tag=tag)
-            nc.scalar.copy(y[c, t][:], banks[c, t][:, 0:CHUNK])
+        def unload(key, source, count, tag):
+            y[key] = keep.tile([P, count], F32, name="y", tag=tag, align_bytes=64)
+            nc.scalar.copy(y[key][:], source)
 
-        merge(0, (0, 1))
-        merge(0, (2, 3))
-        regroup(0)
-        nc.vector.quantize_mx(
-            out=w2_codes[:].bitcast(FP8X4),
-            scales=w2_planes[:],
-            in_=w2_grouped[:].rearrange("p t m j -> p (t m j)"),
-        )
-        merge(1, (0, 1))
-        second_product(0)
+        prepare_w1(2)
+        prepare_w1(3)
+        pick(0, 0, V, ("first0", "w1_grouped3"))
+        for t in range(1, PACK):
+            hidden_rows(t)
+        pick(1, 0, V, ("first1", "second1"))
+        pick(2, 0, EARLY, ("first2a", "second2a"))
+        pick(3, 0, EARLY, ("first3a", "second3a"))
+        add_turned(0, range(PACK))
+        prepare_w2(0)
+        early = regroup(0, 1, "early", "bank4")
+        prepare_w2(1)
+        pick(2, EARLY, LATE, ("first3a", "second3a"))
+        early_bank = psum.tile([P, PACK, EARLY], F32, name="early_bank", tag="bank1")
         for t in order:
-            unload(0, t, "y0_%d" % t)
-        merge(1, (2, 3))
-        regroup(1)
+            second_product(early_bank[:, t, :], t, early)
+        for t in order:
+            unload((0, t), early_bank[:, t, :], EARLY, "y0_%d" % t)
+        for block in range(1, V // P):
+            add_turned(block, range(PACK - 1))
+        pick(3, EARLY, LATE, ("early_grouped", "early_rounded0"))
+        for block in range(1, V // P):
+            add_turned(block, (PACK - 1,))
 
-        window = [keep.tile([P, S], F32, name="window%d" % t) for t in range(PACK)]
+        window = {}
         out_rows = out_0.rearrange("(p t) c -> p t c", t=PACK)
         out_grouped = keep.tile([P, S, PACK], BF16, name="out_grouped", align_bytes=64)
+        spans = ((0, EARLY), (EARLY, LATE))
 
-        def scatter(c, t):
-            pairs = slice(CHUNK * c, CHUNK * (c + 1))
-            nc.vector.tensor_copy(window[t][:].indirect(entries(ka_sb, CHUNK * c, CHUNK)), y[c, t][:])
+        def scatter_first(c, t):
+            start, count = spans[c]
+            nc.vector.tensor_copy(window[t][:].indirect(entries(ka_sb, start, count)), y[c, t][:])
+
+        def scatter_second(c, t):
+            start, count = spans[c]
             nc.vector.tensor_tensor(
-                window[t][:].indirect(entries(kb_sb, CHUNK * c, CHUNK)), y[c, t][:], back_sb[:, pairs], MULT
+                window[t][:].indirect(entries(kb_sb, start, count)), y[c, t][:], back_sb[:, start : start + count], MULT
             )
 
-        scatter(0, order[0])
-        second_product(1)
-        for t in order[:-1]:
-            unload(1, t, "y1_%d" % t)
-        scatter(0, order[1])
+        a, b, c, d = order
+        for t in (a, b, d):
+            window[t] = keep.tile([P, S], F32, name="window%d" % t)
+            scatter_first(0, t)
+        for t in (a, b, d):
+            scatter_second(0, t)
+        middle = regroup(1, 1, "middle", "bank2")
+        late = regroup(2, 2, "late", "bank3")
+        late_banks = {}
         for n, t in enumerate(order):
-            if n >= 2:
-                scatter(0, t)
-            scatter(1, t)
+            late_banks[t] = psum.tile([P, LATE], F32, name="late_bank", tag="bank%d" % (0, 5, 7, 1)[n])
+            second_product(late_banks[t][:, 0:P], t, middle)
+            second_product(late_banks[t][:, P:LATE], t, late)
+            if t != d:
+                unload((1, t), late_banks[t][:], LATE, "y1_%d" % t)
+        window[c] = keep.tile([P, S], F32, name="window", tag="late_grouped", align_bytes=64)
+        scatter_first(0, c)
+        scatter_second(0, c)
+
+        def finish(t):
             nc.sync.dma_start(out=out_rows[:, t, :], in_=window[t][:])
-            if n == 1:
-                unload(1, order[-1], "y1_%d" % t)
-            if n < PACK - 1:
+            if t != d:
                 nc.scalar.copy(out_grouped[:, :, t], window[t][:])
 
-        last = order[-1]
+        scatter_first(1, a)
+        scatter_first(1, b)
+        scatter_second(1, a)
+        finish(a)
+        unload((1, d), late_banks[d][:], LATE, "y1_%d" % a)
+        scatter_first(1, c)
+        scatter_second(1, b)
+        finish(b)
+        scatter_second(1, c)
+        finish(c)
+        scatter_first(1, d)
+        scatter_second(1, d)
+        finish(d)
+
         quarter = S // 4
         out_codes = keep.tile([P, S], U32, name="out_codes", align_bytes=64)
         out_planes = keep.tile([P, S], U8, name="out_planes", align_bytes=64)
         for j in range(4):
             cols = slice(quarter * j, quarter * (j + 1))
             if j < 2:
-                nc.vector.tensor_copy(out_grouped[:, cols, last], window[last][:, cols])
+                nc.vector.tensor_copy(out_grouped[:, cols, d], window[d][:, cols])
             else:
-                nc.scalar.copy(out_grouped[:, cols, last], window[last][:, cols])
+                nc.scalar.copy(out_grouped[:, cols, d], window[d][:, cols])
         words_out = out_1[0].rearrange("p n t -> p (n t)").bitcast(I32)
         for j in range(4):
             cols = slice(quarter * j, quarter * (j + 1))
-            nc.vector.quantize_mx(
-                out=out_codes[:, cols].bitcast(FP8X4),
-                scales=out_planes[:, cols],
-                in_=out_grouped[:, cols, :].rearrange("p c t -> p (c t)"),
-            )
+            quantize(out_codes[:, cols], out_planes[:, cols], out_grouped[:, cols, :].rearrange("p c t -> p (c t)"))
             if j % 2 == 1:
                 both = slice(quarter * (j - 1), quarter * (j + 1))
                 nc.sync.dma_start(out=words_out[:, both], in_=out_codes[:, both].bitcast(I32))

@@ -14,8 +14,8 @@ U16 = mybir.dt.uint16
 U8 = mybir.dt.uint8
 FP8X4 = mybir.dt.float8_e4m3fn_x4
 MULT = mybir.AluOpType.mult
-MAX = mybir.AluOpType.max
 RELU = mybir.ActivationFunctionType.Relu
+COPY = mybir.ActivationFunctionType.Copy
 
 P = 128
 PACK = 4
@@ -23,8 +23,7 @@ K_PASS = P * PACK
 BANK = 512
 LIST_ROWS = 16
 PASSES = K // K_PASS
-EARLY = 128
-LATE = V - EARLY
+HALF = V // 2
 
 
 def tile_picked_zunm_relu_po_kernel(
@@ -42,9 +41,6 @@ def tile_picked_zunm_relu_po_kernel(
         def quantize(codes, planes, grouped):
             nc.vector.quantize_mx(out=codes.bitcast(FP8X4), scales=planes, in_=grouped)
 
-        def interleave(copy, grouped, raw):
-            copy(grouped.rearrange("p (a i) j -> p a j i", i=4), raw.rearrange("p j (a i) -> p a j i", i=4))
-
         offs_sb = keep.tile([P, S // LIST_ROWS], U16, name="offs_sb")
         ka_sb = keep.tile([P, V // LIST_ROWS], U16, name="ka_sb")
         kb_sb = keep.tile([P, V // LIST_ROWS], U16, name="kb_sb")
@@ -52,8 +48,7 @@ def tile_picked_zunm_relu_po_kernel(
         table_scales = keep.tile([P, T], U8, name="table_scales", tag="scales_then_codes", align_bytes=64)
         w1_parts = ((0, P), (P, P), (2 * P, 2 * P))
         w1_raw = [
-            [keep.tile([P, PACK, width], F32, name="w1_raw%d_%d" % (n, o)) for o in range(PASSES)]
-            for n, (first, width) in enumerate(w1_parts)
+            keep.tile([P, PASSES, PACK, width], F32, name="w1_raw%d" % n) for n, (first, width) in enumerate(w1_parts)
         ]
         w2_raw = keep.tile([P, PACK, N], F32, name="w2_raw")
         gate_sb = keep.tile([P, V], F32, name="gate_sb")
@@ -71,7 +66,7 @@ def tile_picked_zunm_relu_po_kernel(
         def load_w1(n):
             first, width = w1_parts[n]
             for o in range(PASSES):
-                nc.sync.dma_start(out=w1_raw[n][o][:], in_=w1_rows[o][:, :, first : first + width])
+                nc.sync.dma_start(out=w1_raw[n][:, o], in_=w1_rows[o][:, :, first : first + width])
 
         nc.vector.memset(table_scales[:].bitcast(I32), 0)
         make_identity(nc, identity[:])
@@ -99,27 +94,31 @@ def tile_picked_zunm_relu_po_kernel(
 
         w1_codes = [keep.tile([P, PASSES, P], U32, name="w1_codes%d" % t, align_bytes=64) for t in range(PACK)]
         w1_planes = [keep.tile([P, PASSES, P], U8, name="w1_planes%d" % t, align_bytes=64) for t in range(PACK)]
+        w1_grouped = {}
         h = {}
-        h_slots = ("w1_raw1_1", "w1_raw2_1", "h2", "h3")
         halves = S // BANK
         acc = {}
 
-        def prepare_w1(t):
+        def group_w1(t, copy):
             n = min(t, 2)
             first = P * t - w1_parts[n][0]
-            grouped = keep.tile([P, PASSES, P, PACK], BF16, name="w1_grouped%d" % t, align_bytes=64)
-            for o in range(PASSES):
-                interleave(nc.scalar.copy, grouped[:, o], w1_raw[n][o][:, :, first : first + P])
+            w1_grouped[t] = keep.tile([P, PASSES, P, PACK], BF16, name="w1_grouped%d" % t, align_bytes=64)
+            copy(
+                w1_grouped[t][:].rearrange("p o (a i) j -> p o a j i", i=4),
+                w1_raw[n][:, :, :, first : first + P].rearrange("p o j (a i) -> p o a j i", i=4),
+            )
+
+        def quantize_w1(t):
             quantize(
                 w1_codes[t][:].rearrange("p o m -> p (o m)"),
                 w1_planes[t][:].rearrange("p o m -> p (o m)"),
-                grouped[:].rearrange("p o m j -> p (o m j)"),
+                w1_grouped[t][:].rearrange("p o m j -> p (o m j)"),
             )
 
         def first_product(o, t, half):
             tokens = slice(BANK * half, BANK * (half + 1))
             if o == 0:
-                acc[t, half] = psum.tile([P, BANK], F32, name="acc", tag="bank%d" % (halves * t + half))
+                acc[t, half] = psum.tile([P, BANK], F32, name="acc", tag="bank%d" % (halves * (t % 2) + half))
             nc.tensor.matmul_mx(
                 out=acc[t, half][:],
                 lhsT=w1_codes[t][:, o, :].bitcast(FP8X4),
@@ -130,16 +129,49 @@ def tile_picked_zunm_relu_po_kernel(
                 stop=(o == PASSES - 1),
             )
 
+        def products(t):
+            for half in range(halves):
+                for o in range(PASSES):
+                    first_product(o, t, half)
+
         def relu(t, half):
             tokens = slice(BANK * half, BANK * (half + 1))
             if half == 0:
-                h[t] = keep.tile([P, S], F32, name="h", tag=h_slots[t])
-            if (t, half) == (0, halves - 1):
-                nc.vector.tensor_scalar(h[t][:, tokens], acc[t, half][:], 0.0, None, MAX)
-            else:
-                nc.scalar.activation(h[t][:, tokens], acc[t, half][:], RELU)
+                h[t] = keep.tile([P, S], F32, name="h%d" % t)
+            nc.scalar.activation(h[t][:, tokens], acc[t, half][:], RELU)
 
-        prepare_w1(0)
+        rounded = keep.tile([P, V // P, 2, P, 2], BF16, name="rounded", align_bytes=64)
+        picked = {}
+
+        def pick(t, start, count):
+            first = keep.tile([P, count], F32, name="first%d_%d" % (t, start), align_bytes=64)
+            second = keep.tile([P, count], F32, name="second%d_%d" % (t, start), align_bytes=64)
+            nc.scalar.activation(first[:], h[t][:].indirect(entries(ka_sb, start, count)), COPY)
+            nc.vector.tensor_tensor(
+                second[:], h[t][:].indirect(entries(kb_sb, start, count)), gate_sb[:, start : start + count], MULT
+            )
+            picked[t, start] = (first, second)
+
+        turned = {}
+
+        def add_turned(t, start, count, bank):
+            first, second = picked[t, start]
+            turned[t, start] = psum.tile([P, count // P, P], F32, name="turned", tag=bank)
+            for b in range(count // P):
+                cols = slice(P * b, P * (b + 1))
+                target = turned[t, start][:, b, :]
+                nc.tensor.matmul(target, first[:, cols], identity[:], start=True, stop=False, is_transpose=True)
+                nc.tensor.matmul(target, second[:, cols], identity[:], start=False, stop=True, is_transpose=True)
+
+        def round_turned(t, start, count, copy):
+            blocks = slice(start // P, (start + count) // P)
+            copy(
+                rounded[:, blocks, :, 32 * t : 32 * (t + 1), :],
+                turned[t, start][:].rearrange("v b (p u e) -> v b u p e", u=2, e=2),
+            )
+
+        group_w1(0, nc.scalar.copy)
+        quantize_w1(0)
         for half in range(halves):
             first_product(0, 0, half)
         x_codes.append(keep.tile([P, S], U32, name="x_codes1", tag="scales_then_codes", align_bytes=64))
@@ -147,188 +179,112 @@ def tile_picked_zunm_relu_po_kernel(
             tokens = slice(BANK * half, BANK * (half + 1))
             nc.vector.tensor_copy(x_codes[1][:, tokens], table[1][:].indirect(entries(offs_sb, BANK * half, BANK)))
             first_product(1, 0, half)
-        prepare_w1(1)
-        for half in range(halves):
             relu(0, half)
 
-        def hidden_rows(t):
+        w2_grouped = keep.tile([P, PACK, P, PACK], BF16, name="w2_grouped", align_bytes=64)
+        w2_codes = keep.tile([P, PACK, P], U32, name="w2_codes", align_bytes=64)
+        w2_planes = keep.tile([P, PACK, P], U8, name="w2_planes", align_bytes=64)
+
+        for t in range(PACK - 1):
+            group_w1(t + 1, nc.vector.tensor_copy)
+            quantize_w1(t + 1)
+            products(t + 1)
+            pick(t, 0, V)
             for half in range(halves):
-                for o in range(PASSES):
-                    first_product(o, t, half)
-                relu(t, half)
+                relu(t + 1, half)
+            add_turned(t, 0, V, "bank%d" % (4 + t % 2))
+            round_turned(t, 0, V, nc.scalar.copy)
+        nc.vector.tensor_copy(
+            w2_grouped[:].rearrange("p t m j -> p m t j"), w2_raw[:].rearrange("p j (m t) -> p m t j", t=PACK)
+        )
+        last = PACK - 1
+        for c in range(2):
+            pick(last, HALF * c, HALF)
+            add_turned(last, HALF * c, HALF, "bank%d" % (5 - c))
+        quantize(
+            w2_codes[:].rearrange("p t m -> p (t m)"),
+            w2_planes[:].rearrange("p t m -> p (t m)"),
+            w2_grouped[:].rearrange("p t m j -> p (t m j)"),
+        )
 
-        z_turned = {}
-        picked = {}
-
-        def pick(t, start, count, tags):
-            first = keep.tile([P, count], F32, name="first", tag=tags[0], align_bytes=64)
-            second = keep.tile([P, count], F32, name="second", tag=tags[1], align_bytes=64)
-            nc.vector.tensor_copy(first[:], h[t][:].indirect(entries(ka_sb, start, count)))
-            nc.vector.tensor_tensor(
-                second[:], h[t][:].indirect(entries(kb_sb, start, count)), gate_sb[:, start : start + count], MULT
-            )
-            for b in range(count // P):
-                cols = slice(P * b, P * (b + 1))
-                picked[t, start // P + b] = (first[:, cols], second[:, cols])
-
-        def add_turned(block, tiles):
-            if block not in z_turned:
-                z_turned[block] = psum.tile([P, H], F32, name="z_turned", tag="bank%d" % (6, 7, 4, 6)[block])
-            for t in tiles:
-                first, second = picked[t, block]
-                target = z_turned[block][:, P * t : P * (t + 1)]
-                nc.tensor.matmul(target, first, identity[:], start=True, stop=False, is_transpose=True)
-                nc.tensor.matmul(target, second, identity[:], start=False, stop=True, is_transpose=True)
-
-        def regroup(first_block, count, name, bank):
-            words = psum.tile([P, count, 2, P], F32, name="words", tag=bank)
-            grouped = keep.tile([P, count * P, PACK], BF16, name="grouped", tag=name + "_grouped", align_bytes=64)
-            for b in range(count):
-                rounded = keep.tile([P, 2, P, 2], BF16, name="rounded", tag=name + "_rounded%d" % b, align_bytes=64)
-                nc.scalar.copy(rounded[:], z_turned[first_block + b][:].rearrange("v (p u e) -> v u p e", u=2, e=2))
+        z_grouped = {}
+        words = {}
+        for c in range(2):
+            round_turned(last, HALF * c, HALF, nc.scalar.copy)
+            words[c] = psum.tile([P, 2, 2, P], F32, name="words", tag="bank%d" % (6 + c))
+            for b in range(2):
                 for u in range(2):
-                    nc.tensor.transpose(words[:, b, u, :], rounded[:, u].rearrange("v p e -> v (p e)").bitcast(F32), identity[:])
-            nc.scalar.copy(
-                grouped[:].rearrange("p v t -> p (v t)").bitcast(F32).rearrange("p (b v u) -> p b v u", b=count, u=2),
-                words[:].rearrange("p b u v -> p b v u"),
-            )
-            codes = keep.tile([P, count * P], U32, name="codes", tag=name + "_codes", align_bytes=64)
-            planes = keep.tile([P, count * P], U8, name="planes", tag=name + "_planes", align_bytes=64)
-            quantize(codes[:], planes[:], grouped[:].rearrange("p v t -> p (v t)"))
-            return codes, planes
-
-        order = (0, 2, 3, 1)
-        w2_codes = {}
-        w2_planes = {}
-
-        def prepare_w2(odd):
-            grouped = keep.tile([P, 2, P, PACK], BF16, name="w2_grouped%d" % odd, align_bytes=64)
-            codes = keep.tile([P, 2, P], U32, name="w2_codes%d" % odd, align_bytes=64)
-            planes = keep.tile([P, 2, P], U8, name="w2_planes%d" % odd, align_bytes=64)
-            nc.scalar.copy(
-                grouped[:].rearrange("p s m j -> p m j s"),
-                w2_raw[:].rearrange("p j (m s e) -> p e m j s", s=2, e=2)[:, odd],
-            )
-            quantize(
-                codes[:].rearrange("p s m -> p (s m)"),
-                planes[:].rearrange("p s m -> p (s m)"),
-                grouped[:].rearrange("p s m j -> p (s m j)"),
-            )
-            for s in range(2):
-                w2_codes[2 * s + odd] = codes[:, s, :]
-                w2_planes[2 * s + odd] = planes[:, s, :]
-
-        def second_product(target, t, operand):
-            codes, planes = operand
-            nc.tensor.matmul_mx(
-                out=target,
-                lhsT=w2_codes[t].bitcast(FP8X4),
-                lhsT_scale=w2_planes[t],
-                rhs=codes[:].bitcast(FP8X4),
-                rhs_scale=planes[:],
-                start=True,
-                stop=True,
-            )
-
+                    nc.tensor.transpose(
+                        words[c][:, b, u, :],
+                        rounded[:, 2 * c + b, u].rearrange("v p e -> v (p e)").bitcast(F32),
+                        identity[:],
+                    )
         y = {}
+        for c in range(2):
+            z_grouped[c] = keep.tile([P, HALF, PACK], BF16, name="z_grouped%d" % c, align_bytes=64)
+            (nc.vector.tensor_copy, nc.scalar.copy)[c](
+                z_grouped[c][:].rearrange("p v t -> p (v t)").bitcast(F32).rearrange("p (b v u) -> p b v u", b=2, u=2),
+                words[c][:].rearrange("p b u v -> p b v u"),
+            )
+        for c in range(2):
+            codes = keep.tile([P, HALF], U32, name="z_codes%d" % c, align_bytes=64)
+            planes = keep.tile([P, HALF], U8, name="z_planes%d" % c, align_bytes=64)
+            quantize(codes[:], planes[:], z_grouped[c][:].rearrange("p v t -> p (v t)"))
+            for pair in range(2):
+                bank = psum.tile([P, 2, HALF], F32, name="y_bank", tag="bank%d" % (2 * c + pair))
+                for s in range(2):
+                    nc.tensor.matmul_mx(
+                        out=bank[:, s, :],
+                        lhsT=w2_codes[:, 2 * pair + s, :].bitcast(FP8X4),
+                        lhsT_scale=w2_planes[:, 2 * pair + s, :],
+                        rhs=codes[:].bitcast(FP8X4),
+                        rhs_scale=planes[:],
+                        start=True,
+                        stop=True,
+                    )
+                unloaded = keep.tile([P, 2, HALF], F32, name="y%d_%d" % (c, pair), align_bytes=64)
+                (nc.scalar.copy, nc.vector.tensor_copy)[pair](unloaded[:], bank[:])
+                for s in range(2):
+                    y[c, 2 * pair + s] = unloaded[:, s, :]
 
-        def unload(key, source, count, tag):
-            y[key] = keep.tile([P, count], F32, name="y", tag=tag, align_bytes=64)
-            nc.scalar.copy(y[key][:], source)
-
-        prepare_w1(2)
-        prepare_w1(3)
-        pick(0, 0, V, ("first0", "w1_grouped3"))
-        for t in range(1, PACK):
-            hidden_rows(t)
-        pick(1, 0, V, ("first1", "second1"))
-        pick(2, 0, EARLY, ("first2a", "second2a"))
-        pick(3, 0, EARLY, ("first3a", "second3a"))
-        add_turned(0, range(PACK))
-        prepare_w2(0)
-        early = regroup(0, 1, "early", "bank4")
-        prepare_w2(1)
-        pick(2, EARLY, LATE, ("first3a", "second3a"))
-        early_bank = psum.tile([P, PACK, EARLY], F32, name="early_bank", tag="bank1")
-        for t in order:
-            second_product(early_bank[:, t, :], t, early)
-        for t in order:
-            unload((0, t), early_bank[:, t, :], EARLY, "y0_%d" % t)
-        for block in range(1, V // P):
-            add_turned(block, range(PACK - 1))
-        pick(3, EARLY, LATE, ("early_grouped", "early_rounded0"))
-        for block in range(1, V // P):
-            add_turned(block, (PACK - 1,))
-
-        window = {}
+        window = [keep.tile([P, S], F32, name="window%d" % t) for t in range(PACK)]
         out_rows = out_0.rearrange("(p t) c -> p t c", t=PACK)
+        out_rounded = keep.tile([P, PACK, S], BF16, name="out_rounded", align_bytes=64)
         out_grouped = keep.tile([P, S, PACK], BF16, name="out_grouped", align_bytes=64)
-        spans = ((0, EARLY), (EARLY, LATE))
 
         def scatter_first(c, t):
-            start, count = spans[c]
-            nc.vector.tensor_copy(window[t][:].indirect(entries(ka_sb, start, count)), y[c, t][:])
+            nc.scalar.activation(window[t][:].indirect(entries(ka_sb, HALF * c, HALF)), y[c, t], COPY)
 
         def scatter_second(c, t):
-            start, count = spans[c]
             nc.vector.tensor_tensor(
-                window[t][:].indirect(entries(kb_sb, start, count)), y[c, t][:], back_sb[:, start : start + count], MULT
+                window[t][:].indirect(entries(kb_sb, HALF * c, HALF)), y[c, t], back_sb[:, HALF * c : HALF * (c + 1)], MULT
             )
 
-        a, b, c, d = order
-        for t in (a, b, d):
-            window[t] = keep.tile([P, S], F32, name="window%d" % t)
+        for t in range(PACK):
             scatter_first(0, t)
-        for t in (a, b, d):
-            scatter_second(0, t)
-        middle = regroup(1, 1, "middle", "bank2")
-        late = regroup(2, 2, "late", "bank3")
-        late_banks = {}
-        for n, t in enumerate(order):
-            late_banks[t] = psum.tile([P, LATE], F32, name="late_bank", tag="bank%d" % (0, 5, 7, 1)[n])
-            second_product(late_banks[t][:, 0:P], t, middle)
-            second_product(late_banks[t][:, P:LATE], t, late)
-            if t != d:
-                unload((1, t), late_banks[t][:], LATE, "y1_%d" % t)
-        window[c] = keep.tile([P, S], F32, name="window", tag="late_grouped", align_bytes=64)
-        scatter_first(0, c)
-        scatter_second(0, c)
-
-        def finish(t):
-            nc.sync.dma_start(out=out_rows[:, t, :], in_=window[t][:])
-            if t != d:
-                nc.scalar.copy(out_grouped[:, :, t], window[t][:])
-
-        scatter_first(1, a)
-        scatter_first(1, b)
-        scatter_second(1, a)
-        finish(a)
-        unload((1, d), late_banks[d][:], LATE, "y1_%d" % a)
-        scatter_first(1, c)
-        scatter_second(1, b)
-        finish(b)
-        scatter_second(1, c)
-        finish(c)
-        scatter_first(1, d)
-        scatter_second(1, d)
-        finish(d)
+            scatter_second(0, (t + 2) % PACK)
+        for t in range(PACK):
+            scatter_first(1, t)
+            scatter_second(1, t ^ 1)
+            if t % 2 == 1:
+                for done, copy in ((t - 1, nc.vector.tensor_copy), (t, nc.scalar.copy)):
+                    nc.sync.dma_start(out=out_rows[:, done, :], in_=window[done][:])
+                    copy(out_rounded[:, done, :], window[done][:])
 
         quarter = S // 4
         out_codes = keep.tile([P, S], U32, name="out_codes", align_bytes=64)
         out_planes = keep.tile([P, S], U8, name="out_planes", align_bytes=64)
-        for j in range(4):
-            cols = slice(quarter * j, quarter * (j + 1))
-            if j < 2:
-                nc.vector.tensor_copy(out_grouped[:, cols, d], window[d][:, cols])
-            else:
-                nc.scalar.copy(out_grouped[:, cols, d], window[d][:, cols])
         words_out = out_1[0].rearrange("p n t -> p (n t)").bitcast(I32)
         for j in range(4):
             cols = slice(quarter * j, quarter * (j + 1))
+            (nc.vector.tensor_copy, nc.scalar.copy)[j % 2](
+                out_grouped[:, cols, :].rearrange("p (a i) t -> p a t i", i=4),
+                out_rounded[:, :, cols].rearrange("p t (a i) -> p a t i", i=4),
+            )
+        for j in (0, 2, 1, 3):
+            cols = slice(quarter * j, quarter * (j + 1))
             quantize(out_codes[:, cols], out_planes[:, cols], out_grouped[:, cols, :].rearrange("p c t -> p (c t)"))
-            if j % 2 == 1:
-                both = slice(quarter * (j - 1), quarter * (j + 1))
-                nc.sync.dma_start(out=words_out[:, both], in_=out_codes[:, both].bitcast(I32))
+            nc.sync.dma_start(out=words_out[:, cols], in_=out_codes[:, cols].bitcast(I32))
         for q in range(4):
             queue = nc.scalar if q % 2 else nc.sync
             queue.dma_start(

@@ -1,7 +1,6 @@
 from contextlib import ExitStack
 
 import concourse.mybir as mybir
-from concourse.masks import make_identity
 
 K, T, S, H, N, V = 1024, 4096, 1024, 512, 512, 512
 FLOPS = 2 * K * H * S + 2 * H * N * V
@@ -13,6 +12,8 @@ U32 = mybir.dt.uint32
 U16 = mybir.dt.uint16
 U8 = mybir.dt.uint8
 FP8X4 = mybir.dt.float8_e4m3fn_x4
+ADD = mybir.AluOpType.add
+MAX = mybir.AluOpType.max
 MULT = mybir.AluOpType.mult
 RELU = mybir.ActivationFunctionType.Relu
 COPY = mybir.ActivationFunctionType.Copy
@@ -24,6 +25,7 @@ BANK = 512
 LIST_ROWS = 16
 PASSES = K // K_PASS
 HALF = V // 2
+RUN = 8
 
 
 def tile_picked_zunm_relu_po_kernel(
@@ -33,6 +35,7 @@ def tile_picked_zunm_relu_po_kernel(
 
     with ExitStack() as ctx:
         keep = ctx.enter_context(tc.tile_pool(name="keep", bufs=1))
+        shared = ctx.enter_context(tc.tile_pool(name="shared", bufs=1))
         psum = ctx.enter_context(tc.psum_pool(name="psum", bufs=1))
 
         def entries(list_tile, start, count):
@@ -44,16 +47,18 @@ def tile_picked_zunm_relu_po_kernel(
         offs_sb = keep.tile([P, S // LIST_ROWS], U16, name="offs_sb")
         ka_sb = keep.tile([P, V // LIST_ROWS], U16, name="ka_sb")
         kb_sb = keep.tile([P, V // LIST_ROWS], U16, name="kb_sb")
-        table = [keep.tile([P, T], U32, name="table%d" % o) for o in range(PASSES)]
-        table_scales = keep.tile([P, T], U8, name="table_scales", tag="scales_then_codes", align_bytes=64)
-        w1_parts = ((0, P), (P, P), (2 * P, 2 * P))
-        w1_raw = [
-            keep.tile([P, PASSES, PACK, width], F32, name="w1_raw%d" % n) for n, (first, width) in enumerate(w1_parts)
+        table = [
+            keep.tile([P, T], U32, name="table0"),
+            shared.tile([P, T], U32, name="table1", offset=0, align_bytes=64),
         ]
+        table_scales = shared.tile([P, T], U8, name="table_scales", offset=16384, align_bytes=64)
+        w1_raw = [keep.tile([P, PACK, H], F32, name="w1_raw%d" % o) for o in range(PASSES)]
         w2_raw = keep.tile([P, PACK, N], F32, name="w2_raw")
-        gate_sb = keep.tile([P, V], F32, name="gate_sb")
+        gate_sb = [
+            keep.tile([P, HALF], F32, name="gate0", tag="gate_then_first", align_bytes=64),
+            keep.tile([P, HALF], F32, name="gate1"),
+        ]
         back_sb = keep.tile([P, V], F32, name="back_sb")
-        identity = keep.tile([P, P], F32, name="identity")
 
         def load_table(o, pieces):
             words = x_words[o].rearrange("p n t -> p (n t)").bitcast(I32)
@@ -61,15 +66,7 @@ def tile_picked_zunm_relu_po_kernel(
                 cols = slice(c * T // pieces, (c + 1) * T // pieces)
                 nc.sync.dma_start(out=table[o][:, cols].bitcast(I32), in_=words[:, cols])
 
-        w1_rows = w1.rearrange("(o p j) c -> o p j c", o=PASSES, j=PACK)
-
-        def load_w1(n):
-            first, width = w1_parts[n]
-            for o in range(PASSES):
-                nc.sync.dma_start(out=w1_raw[n][:, o], in_=w1_rows[o][:, :, first : first + width])
-
         nc.vector.memset(table_scales[:].bitcast(I32), 0)
-        make_identity(nc, identity[:])
         nc.sync.dma_start(offs_sb[:], offs)
         nc.sync.dma_start(kb_sb[:], kb)
         nc.sync.dma_start(ka_sb[:], ka)
@@ -79,12 +76,15 @@ def tile_picked_zunm_relu_po_kernel(
                 out=table_scales[32 * q : 32 * q + 4 * PASSES, :].bitcast(I32),
                 in_=x_scales[:, 4 * q : 4 * q + 4, :].bitcast(I32),
             )
-        load_w1(0)
+        w1_rows = w1.rearrange("(o p j) c -> o p j c", o=PASSES, j=PACK)
+        nc.sync.dma_start(out=w1_raw[0][:], in_=w1_rows[0])
         load_table(1, 1)
-        load_w1(1)
-        nc.sync.dma_start(out=gate_sb[:], in_=gate)
-        load_w1(2)
-        nc.sync.dma_start(out=w2_raw[:], in_=w2.rearrange("(p j) c -> p j c", j=PACK))
+        nc.sync.dma_start(out=w1_raw[1][:], in_=w1_rows[1])
+        for c in range(2):
+            nc.sync.dma_start(out=gate_sb[c][:], in_=gate[:, HALF * c : HALF * (c + 1)])
+        w2_rows = w2.rearrange("(g j r) c -> j g r c", j=PACK, r=RUN)
+        for j in range(PACK):
+            nc.sync.dma_start(out=w2_raw[:, j, :], in_=w2_rows[j])
         nc.sync.dma_start(out=back_sb[:], in_=back)
 
         x_codes = [keep.tile([P, S], U32, name="x_codes0", align_bytes=64)]
@@ -92,164 +92,164 @@ def tile_picked_zunm_relu_po_kernel(
         nc.vector.tensor_copy(x_codes[0][:], table[0][:].indirect(offs_sb[:]))
         nc.vector.tensor_copy(x_planes[:], table_scales[:].indirect(offs_sb[:]))
 
-        w1_codes = [keep.tile([P, PASSES, P], U32, name="w1_codes%d" % t, align_bytes=64) for t in range(PACK)]
-        w1_planes = [keep.tile([P, PASSES, P], U8, name="w1_planes%d" % t, align_bytes=64) for t in range(PACK)]
         w1_grouped = {}
+        w1_codes = {}
+        w1_planes = {}
         h = {}
         halves = S // BANK
         acc = {}
 
-        def group_w1(t, copy):
-            n = min(t, 2)
-            first = P * t - w1_parts[n][0]
-            w1_grouped[t] = keep.tile([P, PASSES, P, PACK], BF16, name="w1_grouped%d" % t, align_bytes=64)
-            copy(
-                w1_grouped[t][:].rearrange("p o (a i) j -> p o a j i", i=4),
-                w1_raw[n][:, :, :, first : first + P].rearrange("p o j (a i) -> p o a j i", i=4),
-            )
-
-        def quantize_w1(t):
-            quantize(
-                w1_codes[t][:].rearrange("p o m -> p (o m)"),
-                w1_planes[t][:].rearrange("p o m -> p (o m)"),
-                w1_grouped[t][:].rearrange("p o m j -> p (o m j)"),
-            )
-
-        def first_product(o, t, half):
-            tokens = slice(BANK * half, BANK * (half + 1))
+        def group_w1(o, t, copy):
             if o == 0:
-                acc[t, half] = psum.tile([P, BANK], F32, name="acc", tag="bank%d" % (halves * (t % 2) + half))
-            nc.tensor.matmul_mx(
-                out=acc[t, half][:],
-                lhsT=w1_codes[t][:, o, :].bitcast(FP8X4),
-                lhsT_scale=w1_planes[t][:, o, :],
-                rhs=x_codes[o][:, tokens].bitcast(FP8X4),
-                rhs_scale=x_planes[4 * o : P, tokens],
-                start=(o == 0),
-                stop=(o == PASSES - 1),
+                grouped = keep.tile([P, P, PACK], BF16, name="w1_grouped0_%d" % t, align_bytes=64)
+            else:
+                grouped = shared.tile([P, P, PACK], BF16, name="w1_grouped1_%d" % t, offset=1024 * t, align_bytes=64)
+            w1_grouped[o, t] = grouped
+            copy(
+                grouped[:].rearrange("p (g a i) j -> p g a j i", a=2, i=4),
+                w1_raw[o][:].rearrange("p j (g t a i) -> p t g a j i", t=PACK, a=2, i=4)[:, t],
             )
 
-        def products(t):
-            for half in range(halves):
-                for o in range(PASSES):
-                    first_product(o, t, half)
+        def quantize_w1(o, t):
+            n = PACK * o + t
+            w1_codes[o, t] = shared.tile([P, P], U32, name="w1_codes%d" % n, offset=(16384, 4096)[o] + 512 * t, align_bytes=64)
+            w1_planes[o, t] = keep.tile([P, P], U8, name="w1_planes%d" % n, align_bytes=64)
+            quantize(w1_codes[o, t][:], w1_planes[o, t][:], w1_grouped[o, t][:].rearrange("p m j -> p (m j)"))
 
-        def relu(t, half):
+        def first_product(o, t):
+            for half in range(halves):
+                tokens = slice(BANK * half, BANK * (half + 1))
+                if o == 0:
+                    acc[t, half] = psum.tile([P, BANK], F32, name="acc", tag="bank%d" % (halves * t + half))
+                nc.tensor.matmul_mx(
+                    out=acc[t, half][:],
+                    lhsT=w1_codes[o, t][:].bitcast(FP8X4),
+                    lhsT_scale=w1_planes[o, t][:],
+                    rhs=x_codes[o][:, tokens].bitcast(FP8X4),
+                    rhs_scale=x_planes[4 * o : P, tokens],
+                    start=(o == 0),
+                    stop=(o == PASSES - 1),
+                )
+
+        def relu(t, half, on_vector):
             tokens = slice(BANK * half, BANK * (half + 1))
             if half == 0:
-                h[t] = keep.tile([P, S], F32, name="h%d" % t)
-            nc.scalar.activation(h[t][:, tokens], acc[t, half][:], RELU)
+                h[t] = keep.tile([P, S], F32, name="h", tag=("h0", "h1", "h2", "w2_raw")[t])
+            if on_vector:
+                nc.vector.tensor_scalar(h[t][:, tokens], acc[t, half][:], 0.0, None, MAX)
+            else:
+                nc.scalar.activation(h[t][:, tokens], acc[t, half][:], RELU)
 
-        rounded = keep.tile([P, V // P, 2, P, 2], BF16, name="rounded", align_bytes=64)
-        picked = {}
+        for t in range(PACK):
+            group_w1(0, t, nc.scalar.copy)
+            quantize_w1(0, t)
+            first_product(0, t)
+        x_codes.append(shared.tile([P, S], U32, name="x_codes1", offset=16384 + 2048, align_bytes=64))
+        nc.vector.tensor_copy(x_codes[1][:], table[1][:].indirect(offs_sb[:]))
+        group_w1(1, 0, nc.vector.tensor_copy)
+        group_w1(1, 1, nc.vector.tensor_copy)
+        group_w1(1, 2, nc.scalar.copy)
+        group_w1(1, 3, nc.scalar.copy)
+        quantize_w1(1, 0)
+        quantize_w1(1, 1)
+        first_product(1, 0)
+        first_product(1, 1)
+        quantize_w1(1, 2)
+        quantize_w1(1, 3)
+        for t in range(2, PACK):
+            first_product(1, t)
 
-        def pick(t, start, count):
-            first = keep.tile([P, count], F32, name="first%d_%d" % (t, start), align_bytes=64)
-            second = keep.tile([P, count], F32, name="second%d_%d" % (t, start), align_bytes=64)
-            nc.scalar.activation(first[:], h[t][:].indirect(entries(ka_sb, start, count)), COPY)
-            nc.vector.tensor_tensor(
-                second[:], h[t][:].indirect(entries(kb_sb, start, count)), gate_sb[:, start : start + count], MULT
-            )
-            picked[t, start] = (first, second)
+        first = [keep.tile([P, PACK, HALF], F32, name="first0", align_bytes=64)]
+        seconds = keep.tile([P, 2 * PACK - 1, HALF], F32, name="seconds", align_bytes=64)
+        second = [seconds[:, PACK - 1 :, :], seconds[:, :PACK, :]]
 
-        turned = {}
+        def pick_first(c, t):
+            nc.scalar.activation(first[c][:, t, :], h[t][:].indirect(entries(ka_sb, HALF * c, HALF)), COPY)
 
-        def add_turned(t, start, count, bank):
-            first, second = picked[t, start]
-            turned[t, start] = psum.tile([P, count // P, P], F32, name="turned", tag=bank)
-            for b in range(count // P):
-                cols = slice(P * b, P * (b + 1))
-                target = turned[t, start][:, b, :]
-                nc.tensor.matmul(target, first[:, cols], identity[:], start=True, stop=False, is_transpose=True)
-                nc.tensor.matmul(target, second[:, cols], identity[:], start=False, stop=True, is_transpose=True)
-
-        def round_turned(t, start, count, copy):
-            blocks = slice(start // P, (start + count) // P)
-            copy(
-                rounded[:, blocks, :, 32 * t : 32 * (t + 1), :],
-                turned[t, start][:].rearrange("v b (p u e) -> v b u p e", u=2, e=2),
-            )
-
-        group_w1(0, nc.scalar.copy)
-        quantize_w1(0)
-        for half in range(halves):
-            first_product(0, 0, half)
-        x_codes.append(keep.tile([P, S], U32, name="x_codes1", tag="scales_then_codes", align_bytes=64))
-        for half in range(halves):
-            tokens = slice(BANK * half, BANK * (half + 1))
-            nc.vector.tensor_copy(x_codes[1][:, tokens], table[1][:].indirect(entries(offs_sb, BANK * half, BANK)))
-            first_product(1, 0, half)
-            relu(0, half)
+        def pick_second(c, t):
+            nc.vector.tensor_tensor(second[c][:, t, :], h[t][:].indirect(entries(kb_sb, HALF * c, HALF)), gate_sb[c][:], MULT)
 
         w2_grouped = keep.tile([P, PACK, P, PACK], BF16, name="w2_grouped", align_bytes=64)
         w2_codes = keep.tile([P, PACK, P], U32, name="w2_codes", align_bytes=64)
         w2_planes = keep.tile([P, PACK, P], U8, name="w2_planes", align_bytes=64)
 
+        for t in range(PACK):
+            relu(t, 0, False)
+            relu(t, 1, t in (0,))
+            if t == 1:
+                nc.vector.tensor_copy(
+                    w2_grouped[:].rearrange("p t m j -> p m t j"), w2_raw[:].rearrange("p j (m t) -> p m t j", t=PACK)
+                )
+        for t in range(PACK):
+            pick_first(0, t)
         for t in range(PACK - 1):
-            group_w1(t + 1, nc.vector.tensor_copy)
-            quantize_w1(t + 1)
-            products(t + 1)
-            pick(t, 0, V)
-            for half in range(halves):
-                relu(t + 1, half)
-            add_turned(t, 0, V, "bank%d" % (4 + t % 2))
-            round_turned(t, 0, V, nc.scalar.copy)
-        nc.vector.tensor_copy(
-            w2_grouped[:].rearrange("p t m j -> p m t j"), w2_raw[:].rearrange("p j (m t) -> p m t j", t=PACK)
-        )
-        last = PACK - 1
-        for c in range(2):
-            pick(last, HALF * c, HALF)
-            add_turned(last, HALF * c, HALF, "bank%d" % (5 - c))
+            pick_second(0, t)
+            pick_second(1, t)
         quantize(
             w2_codes[:].rearrange("p t m -> p (t m)"),
             w2_planes[:].rearrange("p t m -> p (t m)"),
             w2_grouped[:].rearrange("p t m j -> p (t m j)"),
         )
-
+        pick_second(0, PACK - 1)
         z_grouped = {}
-        words = {}
-        for c in range(2):
-            round_turned(last, HALF * c, HALF, nc.scalar.copy)
-            words[c] = psum.tile([P, 2, 2, P], F32, name="words", tag="bank%d" % (6 + c))
-            for b in range(2):
-                for u in range(2):
-                    nc.tensor.transpose(
-                        words[c][:, b, u, :],
-                        rounded[:, 2 * c + b, u].rearrange("v p e -> v (p e)").bitcast(F32),
-                        identity[:],
-                    )
+        z_codes = {}
+        z_planes = {}
         y = {}
-        for c in range(2):
-            z_grouped[c] = keep.tile([P, HALF, PACK], BF16, name="z_grouped%d" % c, align_bytes=64)
-            (nc.vector.tensor_copy, nc.scalar.copy)[c](
-                z_grouped[c][:].rearrange("p v t -> p (v t)").bitcast(F32).rearrange("p (b v u) -> p b v u", b=2, u=2),
-                words[c][:].rearrange("p b u v -> p b v u"),
+
+        def merge(c):
+            z_grouped[c] = keep.tile([P, HALF, PACK], BF16, name="z_grouped", align_bytes=64)
+            nc.vector.tensor_tensor(
+                z_grouped[c][:].rearrange("p (a i) t -> p a t i", i=4),
+                first[c][:].rearrange("p t (a i) -> p a t i", i=4),
+                second[c].rearrange("p t (a i) -> p a t i", i=4),
+                ADD,
             )
-        for c in range(2):
-            codes = keep.tile([P, HALF], U32, name="z_codes%d" % c, align_bytes=64)
-            planes = keep.tile([P, HALF], U8, name="z_planes%d" % c, align_bytes=64)
-            quantize(codes[:], planes[:], z_grouped[c][:].rearrange("p v t -> p (v t)"))
+
+        def quantize_z(c):
+            z_codes[c] = keep.tile([P, HALF], U32, name="z_codes%d" % c, align_bytes=64)
+            z_planes[c] = keep.tile([P, HALF], U8, name="z_planes%d" % c, align_bytes=64)
+            quantize(z_codes[c][:], z_planes[c][:], z_grouped[c][:].rearrange("p v t -> p (v t)"))
+
+        y_bank = {}
+
+        def second_product(c):
             for pair in range(2):
-                bank = psum.tile([P, 2, HALF], F32, name="y_bank", tag="bank%d" % (2 * c + pair))
+                y_bank[c, pair] = psum.tile([P, 2, HALF], F32, name="y_bank", tag="bank%d" % (2 * c + pair))
                 for s in range(2):
                     nc.tensor.matmul_mx(
-                        out=bank[:, s, :],
+                        out=y_bank[c, pair][:, s, :],
                         lhsT=w2_codes[:, 2 * pair + s, :].bitcast(FP8X4),
                         lhsT_scale=w2_planes[:, 2 * pair + s, :],
-                        rhs=codes[:].bitcast(FP8X4),
-                        rhs_scale=planes[:],
+                        rhs=z_codes[c][:].bitcast(FP8X4),
+                        rhs_scale=z_planes[c][:],
                         start=True,
                         stop=True,
                     )
-                unloaded = keep.tile([P, 2, HALF], F32, name="y%d_%d" % (c, pair), align_bytes=64)
-                (nc.scalar.copy, nc.vector.tensor_copy)[pair](unloaded[:], bank[:])
-                for s in range(2):
-                    y[c, 2 * pair + s] = unloaded[:, s, :]
+
+        def unload(c, pair, copy):
+            unloaded = keep.tile([P, 2, HALF], F32, name="y%d_%d" % (c, pair), align_bytes=64)
+            copy(unloaded[:], y_bank[c, pair][:])
+            for s in range(2):
+                y[c, 2 * pair + s] = unloaded[:, s, :]
+
+        merge(0)
+        quantize_z(0)
+        pick_second(1, PACK - 1)
+        second_product(0)
+        first.append(keep.tile([P, PACK, HALF], F32, name="first1", tag="gate_then_first", align_bytes=64))
+        for t in range(PACK):
+            pick_first(1, t)
+        unload(0, 0, nc.scalar.copy)
+        unload(0, 1, nc.vector.tensor_copy)
+        merge(1)
+        quantize_z(1)
+        second_product(1)
+        unload(1, 0, nc.scalar.copy)
+        unload(1, 1, nc.vector.tensor_copy)
 
         window = [keep.tile([P, S], F32, name="window%d" % t) for t in range(PACK)]
         out_rows = out_0.rearrange("(p t) c -> p t c", t=PACK)
-        out_rounded = keep.tile([P, PACK, S], BF16, name="out_rounded", align_bytes=64)
+        collected = keep.tile([P, PACK, S], F32, name="collected", align_bytes=64)
         out_grouped = keep.tile([P, S, PACK], BF16, name="out_grouped", align_bytes=64)
 
         def scatter_first(c, t):
@@ -260,29 +260,29 @@ def tile_picked_zunm_relu_po_kernel(
                 window[t][:].indirect(entries(kb_sb, HALF * c, HALF)), y[c, t], back_sb[:, HALF * c : HALF * (c + 1)], MULT
             )
 
-        for t in range(PACK):
-            scatter_first(0, t)
-            scatter_second(0, (t + 2) % PACK)
-        for t in range(PACK):
-            scatter_first(1, t)
-            scatter_second(1, t ^ 1)
-            if t % 2 == 1:
-                for done, copy in ((t - 1, nc.vector.tensor_copy), (t, nc.scalar.copy)):
-                    nc.sync.dma_start(out=out_rows[:, done, :], in_=window[done][:])
-                    copy(out_rounded[:, done, :], window[done][:])
+        for c in range(2):
+            for t in range(PACK):
+                scatter_first(c, t)
+                scatter_second(c, t)
+                if c == 1 and t < 2:
+                    nc.sync.dma_start(out=collected[:, t, :], in_=window[t][:])
+                if c == 1:
+                    nc.sync.dma_start(out=out_rows[:, t, :], in_=window[t][:])
+        nc.scalar.copy(collected[:, 2, :], window[2][:])
 
-        quarter = S // 4
         out_codes = keep.tile([P, S], U32, name="out_codes", align_bytes=64)
         out_planes = keep.tile([P, S], U8, name="out_planes", align_bytes=64)
         words_out = out_1[0].rearrange("p n t -> p (n t)").bitcast(I32)
-        for j in range(4):
-            cols = slice(quarter * j, quarter * (j + 1))
-            (nc.vector.tensor_copy, nc.scalar.copy)[j % 2](
-                out_grouped[:, cols, :].rearrange("p (a i) t -> p a t i", i=4),
-                out_rounded[:, :, cols].rearrange("p t (a i) -> p a t i", i=4),
+        spans = ((0, 256, nc.vector.tensor_copy), (640, 1024, nc.scalar.copy), (256, 640, nc.vector.tensor_copy))
+        for start, stop, copy in spans:
+            copy(collected[:, 3, start:stop], window[3][:, start:stop])
+        for start, stop, copy in spans:
+            copy(
+                out_grouped[:, start:stop, :].rearrange("p (a i) t -> p a t i", i=4),
+                collected[:, :, start:stop].rearrange("p t (a i) -> p a t i", i=4),
             )
-        for j in (0, 2, 1, 3):
-            cols = slice(quarter * j, quarter * (j + 1))
+        for start, stop, copy in sorted(spans, key=lambda span: span[0]):
+            cols = slice(start, stop)
             quantize(out_codes[:, cols], out_planes[:, cols], out_grouped[:, cols, :].rearrange("p c t -> p (c t)"))
             nc.sync.dma_start(out=words_out[:, cols], in_=out_codes[:, cols].bitcast(I32))
         for q in range(4):

@@ -36,6 +36,7 @@ def tile_picked_zunm_relu_po_kernel(
     with ExitStack() as ctx:
         keep = ctx.enter_context(tc.tile_pool(name="keep", bufs=1))
         shared = ctx.enter_context(tc.tile_pool(name="shared", bufs=1))
+        after_table0 = ctx.enter_context(tc.tile_pool(name="after_table0", bufs=1))
         psum = ctx.enter_context(tc.psum_pool(name="psum", bufs=1))
 
         def entries(list_tile, start, count):
@@ -47,18 +48,9 @@ def tile_picked_zunm_relu_po_kernel(
         offs_sb = keep.tile([P, S // LIST_ROWS], U16, name="offs_sb")
         ka_sb = keep.tile([P, V // LIST_ROWS], U16, name="ka_sb")
         kb_sb = keep.tile([P, V // LIST_ROWS], U16, name="kb_sb")
-        table = [
-            keep.tile([P, T], U32, name="table0"),
-            shared.tile([P, T], U32, name="table1", offset=0, align_bytes=64),
-        ]
-        table_scales = shared.tile([P, T], U8, name="table_scales", offset=16384, align_bytes=64)
-        w1_raw = [keep.tile([P, PACK, H], F32, name="w1_raw%d" % o) for o in range(PASSES)]
-        w2_raw = keep.tile([P, PACK, N], F32, name="w2_raw")
-        gate_sb = [
-            keep.tile([P, HALF], F32, name="gate0", tag="gate_then_first", align_bytes=64),
-            keep.tile([P, HALF], F32, name="gate1"),
-        ]
-        back_sb = keep.tile([P, V], F32, name="back_sb")
+        table = [after_table0.tile([P, T], U32, name="table0", offset=0, align_bytes=64)]
+        table_scales = shared.tile([P, T], U8, name="table_scales", offset=0, align_bytes=64)
+        w1_raw = [keep.tile([P, PACK, H], F32, name="w1_raw0")]
 
         def load_table(o, pieces):
             words = x_words[o].rearrange("p n t -> p (n t)").bitcast(I32)
@@ -70,15 +62,49 @@ def tile_picked_zunm_relu_po_kernel(
         nc.sync.dma_start(offs_sb[:], offs)
         nc.sync.dma_start(kb_sb[:], kb)
         nc.sync.dma_start(ka_sb[:], ka)
-        load_table(0, 4)
-        for q in range(4):
-            nc.sync.dma_start(
-                out=table_scales[32 * q : 32 * q + 4 * PASSES, :].bitcast(I32),
-                in_=x_scales[:, 4 * q : 4 * q + 4, :].bitcast(I32),
-            )
         w1_rows = w1.rearrange("(o p j) c -> o p j c", o=PASSES, j=PACK)
-        nc.sync.dma_start(out=w1_raw[0][:], in_=w1_rows[0])
+
+        def load_w1_rows(j):
+            for half in range(2):
+                cols = slice(half * H // 2, (half + 1) * H // 2)
+                nc.sync.dma_start(out=w1_raw[0][:, j, cols], in_=w1_rows[0][:, j, cols])
+
+        load_w1_rows(0)
+        load_w1_rows(1)
+        nc.sync.dma_start(
+            out=table_scales[0:P:4, :].bitcast(I32), in_=x_scales.rearrange("o r c -> (o r) c").bitcast(I32)
+        )
+        load_w1_rows(2)
+        load_w1_rows(3)
+        load_table(0, 1)
+
+        picked_scales = keep.tile([P, S], U8, name="picked_scales", align_bytes=64)
+        x_planes = [keep.tile([P, S], U8, name="x_planes%d" % o, align_bytes=64) for o in range(PASSES)]
+        for o in range(PASSES):
+            nc.vector.memset(x_planes[o][:].bitcast(I32), 0)
+        nc.vector.tensor_copy(picked_scales[:], table_scales[:].indirect(offs_sb[:]))
+        x_codes = [keep.tile([P, S], U32, name="x_codes0", align_bytes=64)]
+        nc.vector.tensor_copy(x_codes[0][:], table[0][:].indirect(offs_sb[:]))
+
+        def place_scales(o, quadrants):
+            for q in quadrants:
+                source = 64 * o + 16 * q
+                nc.sync.dma_start(
+                    out=x_planes[o][32 * q : 32 * q + 4, :].bitcast(I32),
+                    in_=picked_scales[source : source + 16 : 4, :].bitcast(I32),
+                )
+
+        place_scales(0, range(4))
+        place_scales(1, range(2))
+        table.append(shared.tile([P, T], U32, name="table1", offset=0, align_bytes=64))
         load_table(1, 1)
+        place_scales(1, range(2, 4))
+        w1_raw.append(after_table0.tile([P, PACK, H], F32, name="w1_raw1", offset=0, align_bytes=64))
+        gate_sb = [
+            after_table0.tile([P, HALF], F32, name="gate%d" % c, offset=8192 + 4096 * c, align_bytes=64) for c in range(2)
+        ]
+        back_sb = after_table0.tile([P, V], F32, name="back_sb", offset=13312, align_bytes=64)
+        w2_raw = after_table0.tile([P, PACK, N], F32, name="w2_raw", offset=15360, align_bytes=64)
         nc.sync.dma_start(out=w1_raw[1][:], in_=w1_rows[1])
         for c in range(2):
             nc.sync.dma_start(out=gate_sb[c][:], in_=gate[:, HALF * c : HALF * (c + 1)])
@@ -86,11 +112,6 @@ def tile_picked_zunm_relu_po_kernel(
         for j in range(PACK):
             nc.sync.dma_start(out=w2_raw[:, j, :], in_=w2_rows[j])
         nc.sync.dma_start(out=back_sb[:], in_=back)
-
-        x_codes = [keep.tile([P, S], U32, name="x_codes0", align_bytes=64)]
-        x_planes = keep.tile([P, S], U8, name="x_planes", align_bytes=64)
-        nc.vector.tensor_copy(x_codes[0][:], table[0][:].indirect(offs_sb[:]))
-        nc.vector.tensor_copy(x_planes[:], table_scales[:].indirect(offs_sb[:]))
 
         w1_grouped = {}
         w1_codes = {}
@@ -112,7 +133,7 @@ def tile_picked_zunm_relu_po_kernel(
 
         def quantize_w1(o, t):
             n = PACK * o + t
-            w1_codes[o, t] = shared.tile([P, P], U32, name="w1_codes%d" % n, offset=(16384, 4096)[o] + 512 * t, align_bytes=64)
+            w1_codes[o, t] = keep.tile([P, P], U32, name="w1_codes%d" % n, align_bytes=64)
             w1_planes[o, t] = keep.tile([P, P], U8, name="w1_planes%d" % n, align_bytes=64)
             quantize(w1_codes[o, t][:], w1_planes[o, t][:], w1_grouped[o, t][:].rearrange("p m j -> p (m j)"))
 
@@ -126,7 +147,7 @@ def tile_picked_zunm_relu_po_kernel(
                     lhsT=w1_codes[o, t][:].bitcast(FP8X4),
                     lhsT_scale=w1_planes[o, t][:],
                     rhs=x_codes[o][:, tokens].bitcast(FP8X4),
-                    rhs_scale=x_planes[4 * o : P, tokens],
+                    rhs_scale=x_planes[o][:, tokens],
                     start=(o == 0),
                     stop=(o == PASSES - 1),
                 )
@@ -134,7 +155,7 @@ def tile_picked_zunm_relu_po_kernel(
         def relu(t, half, on_vector):
             tokens = slice(BANK * half, BANK * (half + 1))
             if half == 0:
-                h[t] = keep.tile([P, S], F32, name="h", tag=("h0", "h1", "h2", "w2_raw")[t])
+                h[t] = keep.tile([P, S], F32, name="h%d" % t)
             if on_vector:
                 nc.vector.tensor_scalar(h[t][:, tokens], acc[t, half][:], 0.0, None, MAX)
             else:
@@ -143,8 +164,9 @@ def tile_picked_zunm_relu_po_kernel(
         for t in range(PACK):
             group_w1(0, t, nc.scalar.copy)
             quantize_w1(0, t)
+        for t in range(PACK):
             first_product(0, t)
-        x_codes.append(shared.tile([P, S], U32, name="x_codes1", offset=16384 + 2048, align_bytes=64))
+        x_codes.append(keep.tile([P, S], U32, name="x_codes1", align_bytes=64))
         nc.vector.tensor_copy(x_codes[1][:], table[1][:].indirect(offs_sb[:]))
         group_w1(1, 0, nc.vector.tensor_copy)
         group_w1(1, 1, nc.vector.tensor_copy)
@@ -169,7 +191,7 @@ def tile_picked_zunm_relu_po_kernel(
         def pick_second(c, t):
             nc.vector.tensor_tensor(second[c][:, t, :], h[t][:].indirect(entries(kb_sb, HALF * c, HALF)), gate_sb[c][:], MULT)
 
-        w2_grouped = keep.tile([P, PACK, P, PACK], BF16, name="w2_grouped", align_bytes=64)
+        w2_grouped = shared.tile([P, PACK, P, PACK], BF16, name="w2_grouped", offset=0, align_bytes=64)
         w2_codes = keep.tile([P, PACK, P], U32, name="w2_codes", align_bytes=64)
         w2_planes = keep.tile([P, PACK, P], U8, name="w2_planes", align_bytes=64)
 
@@ -236,11 +258,11 @@ def tile_picked_zunm_relu_po_kernel(
         quantize_z(0)
         pick_second(1, PACK - 1)
         second_product(0)
-        first.append(keep.tile([P, PACK, HALF], F32, name="first1", tag="gate_then_first", align_bytes=64))
+        first.append(after_table0.tile([P, PACK, HALF], F32, name="first1", offset=8192, align_bytes=64))
         for t in range(PACK):
             pick_first(1, t)
+        unload(0, 1, nc.scalar.copy)
         unload(0, 0, nc.scalar.copy)
-        unload(0, 1, nc.vector.tensor_copy)
         merge(1)
         quantize_z(1)
         second_product(1)
@@ -260,28 +282,37 @@ def tile_picked_zunm_relu_po_kernel(
                 window[t][:].indirect(entries(kb_sb, HALF * c, HALF)), y[c, t], back_sb[:, HALF * c : HALF * (c + 1)], MULT
             )
 
-        for c in range(2):
-            for t in range(PACK):
-                scatter_first(c, t)
-                scatter_second(c, t)
-                if c == 1 and t < 2:
-                    nc.sync.dma_start(out=collected[:, t, :], in_=window[t][:])
-                if c == 1:
-                    nc.sync.dma_start(out=out_rows[:, t, :], in_=window[t][:])
-        nc.scalar.copy(collected[:, 2, :], window[2][:])
+        steps = ((0, 0), (0, 1), (0, 3), (1, 0), (1, 1), (1, 2), (1, 3), (0, 2))
+        behind = steps[-1]
+        for step in steps:
+            scatter_first(*step)
+            scatter_second(*behind)
+            if behind in ((1, 0), (1, 1)):
+                done = behind[1]
+                nc.sync.dma_start(out=collected[:, done, :], in_=window[done][:])
+                nc.sync.dma_start(out=out_rows[:, done, :], in_=window[done][:])
+            behind = step
+        for done in (2, 3):
+            nc.sync.dma_start(out=out_rows[:, done, :], in_=window[done][:])
 
         out_codes = keep.tile([P, S], U32, name="out_codes", align_bytes=64)
         out_planes = keep.tile([P, S], U8, name="out_planes", align_bytes=64)
         words_out = out_1[0].rearrange("p n t -> p (n t)").bitcast(I32)
-        spans = ((0, 256, nc.vector.tensor_copy), (640, 1024, nc.scalar.copy), (256, 640, nc.vector.tensor_copy))
-        for start, stop, copy in spans:
-            copy(collected[:, 3, start:stop], window[3][:, start:stop])
-        for start, stop, copy in spans:
+        split = 576
+        for start, stop, copy in ((0, split, nc.vector.tensor_copy), (split, S, nc.scalar.copy)):
+            for done in (2, 3):
+                copy(collected[:, done, start:stop], window[done][:, start:stop])
+        for start, stop, copy in (
+            (0, 256, nc.vector.tensor_copy),
+            (split, 896, nc.scalar.copy),
+            (256, split, nc.vector.tensor_copy),
+            (896, S, nc.scalar.copy),
+        ):
             copy(
                 out_grouped[:, start:stop, :].rearrange("p (a i) t -> p a t i", i=4),
                 collected[:, :, start:stop].rearrange("p t (a i) -> p a t i", i=4),
             )
-        for start, stop, copy in sorted(spans, key=lambda span: span[0]):
+        for start, stop in ((0, 256), (256, 512), (512, 896), (896, S)):
             cols = slice(start, stop)
             quantize(out_codes[:, cols], out_planes[:, cols], out_grouped[:, cols, :].rearrange("p c t -> p (c t)"))
             nc.sync.dma_start(out=words_out[:, cols], in_=out_codes[:, cols].bitcast(I32))

@@ -58,24 +58,18 @@ def tile_picked_zunm_relu_po_kernel(
                 cols = slice(c * T // pieces, (c + 1) * T // pieces)
                 nc.sync.dma_start(out=table[o][:, cols].bitcast(I32), in_=words[:, cols])
 
-        nc.vector.memset(table_scales[:].bitcast(I32), 0)
+        nc.gpsimd.memset(table_scales[:, : T // 2].bitcast(I32), 0)
+        nc.vector.memset(table_scales[:, T // 2 :].bitcast(I32), 0)
+        w1_rows = w1.rearrange("(o p j) c -> o p j c", o=PASSES, j=PACK)
+        nc.sync.dma_start(out=w1_raw[0][:, 0, :], in_=w1_rows[0][:, 0, :])
         nc.sync.dma_start(offs_sb[:], offs)
         nc.sync.dma_start(kb_sb[:], kb)
         nc.sync.dma_start(ka_sb[:], ka)
-        w1_rows = w1.rearrange("(o p j) c -> o p j c", o=PASSES, j=PACK)
-
-        def load_w1_rows(j):
-            for half in range(2):
-                cols = slice(half * H // 2, (half + 1) * H // 2)
-                nc.sync.dma_start(out=w1_raw[0][:, j, cols], in_=w1_rows[0][:, j, cols])
-
-        load_w1_rows(0)
-        load_w1_rows(1)
+        nc.sync.dma_start(out=w1_raw[0][:, 1, :], in_=w1_rows[0][:, 1, :])
         nc.sync.dma_start(
             out=table_scales[0:P:4, :].bitcast(I32), in_=x_scales.rearrange("o r c -> (o r) c").bitcast(I32)
         )
-        load_w1_rows(2)
-        load_w1_rows(3)
+        nc.sync.dma_start(out=w1_raw[0][:, 2:, :], in_=w1_rows[0][:, 2:, :])
         load_table(0, 1)
 
         picked_scales = keep.tile([P, S], U8, name="picked_scales", align_bytes=64)

@@ -24,7 +24,9 @@ K_PASS = P * PACK
 BANK = 512
 LIST_ROWS = 16
 PASSES = K // K_PASS
-HALF = V // 2
+EARLY = 128
+LATE = V - EARLY
+SPANS = ((0, EARLY), (EARLY, LATE))
 RUN = 8
 
 
@@ -84,7 +86,7 @@ def tile_picked_zunm_relu_po_kernel(
             for q in quadrants:
                 source = 64 * o + 16 * q
                 nc.sync.dma_start(
-                    out=x_planes[o][32 * q : 32 * q + 4, :].bitcast(I32),
+                    out=x_planes[o][32 * q + 4 * o : 32 * q + 4 * o + 4, :].bitcast(I32),
                     in_=picked_scales[source : source + 16 : 4, :].bitcast(I32),
                 )
 
@@ -95,17 +97,18 @@ def tile_picked_zunm_relu_po_kernel(
         place_scales(1, range(2, 4))
         w1_raw.append(after_table0.tile([P, PACK, H], F32, name="w1_raw1", offset=0, align_bytes=64))
         gate_sb = [
-            after_table0.tile([P, HALF], F32, name="gate%d" % c, offset=8192 + 4096 * c, align_bytes=64) for c in range(2)
+            after_table0.tile([P, EARLY], F32, name="gate0", offset=8192, align_bytes=64),
+            after_table0.tile([P, LATE], F32, name="gate1", offset=8704, align_bytes=64),
         ]
-        back_sb = after_table0.tile([P, V], F32, name="back_sb", offset=13312, align_bytes=64)
+        back_sb = {1: after_table0.tile([P, LATE], F32, name="back1", offset=13312, align_bytes=64)}
         w2_raw = after_table0.tile([P, PACK, N], F32, name="w2_raw", offset=15360, align_bytes=64)
         nc.sync.dma_start(out=w1_raw[1][:], in_=w1_rows[1])
-        for c in range(2):
-            nc.sync.dma_start(out=gate_sb[c][:], in_=gate[:, HALF * c : HALF * (c + 1)])
+        for c, (start, count) in enumerate(SPANS):
+            nc.sync.dma_start(out=gate_sb[c][:], in_=gate[:, start : start + count])
         w2_rows = w2.rearrange("(g j r) c -> j g r c", j=PACK, r=RUN)
         for j in range(PACK):
             nc.sync.dma_start(out=w2_raw[:, j, :], in_=w2_rows[j])
-        nc.sync.dma_start(out=back_sb[:], in_=back)
+        nc.sync.dma_start(out=back_sb[1][:], in_=back[:, EARLY:])
 
         w1_grouped = {}
         w1_codes = {}
@@ -141,7 +144,7 @@ def tile_picked_zunm_relu_po_kernel(
                     lhsT=w1_codes[o, t][:].bitcast(FP8X4),
                     lhsT_scale=w1_planes[o, t][:],
                     rhs=x_codes[o][:, tokens].bitcast(FP8X4),
-                    rhs_scale=x_planes[o][:, tokens],
+                    rhs_scale=x_planes[o][4 * o :, tokens],
                     start=(o == 0),
                     stop=(o == PASSES - 1),
                 )
@@ -175,15 +178,19 @@ def tile_picked_zunm_relu_po_kernel(
         for t in range(2, PACK):
             first_product(1, t)
 
-        first = [keep.tile([P, PACK, HALF], F32, name="first0", align_bytes=64)]
-        seconds = keep.tile([P, 2 * PACK - 1, HALF], F32, name="seconds", align_bytes=64)
-        second = [seconds[:, PACK - 1 :, :], seconds[:, :PACK, :]]
+        first = [keep.tile([P, PACK, EARLY], F32, name="first0", align_bytes=64)]
+        seconds = keep.tile([P, PACK * LATE], F32, name="seconds", align_bytes=64)
+        early_start = 2 * LATE - 64
+        second = [
+            seconds[:, early_start : early_start + PACK * EARLY].rearrange("p (t v) -> p t v", t=PACK),
+            seconds[:].rearrange("p (t v) -> p t v", t=PACK),
+        ]
 
         def pick_first(c, t):
-            nc.scalar.activation(first[c][:, t, :], h[t][:].indirect(entries(ka_sb, HALF * c, HALF)), COPY)
+            nc.scalar.activation(first[c][:, t, :], h[t][:].indirect(entries(ka_sb, *SPANS[c])), COPY)
 
         def pick_second(c, t):
-            nc.vector.tensor_tensor(second[c][:, t, :], h[t][:].indirect(entries(kb_sb, HALF * c, HALF)), gate_sb[c][:], MULT)
+            nc.vector.tensor_tensor(second[c][:, t, :], h[t][:].indirect(entries(kb_sb, *SPANS[c])), gate_sb[c][:], MULT)
 
         w2_grouped = shared.tile([P, PACK, P, PACK], BF16, name="w2_grouped", offset=0, align_bytes=64)
         w2_codes = keep.tile([P, PACK, P], U32, name="w2_codes", align_bytes=64)
@@ -200,20 +207,21 @@ def tile_picked_zunm_relu_po_kernel(
             pick_first(0, t)
         for t in range(PACK - 1):
             pick_second(0, t)
-            pick_second(1, t)
         quantize(
             w2_codes[:].rearrange("p t m -> p (t m)"),
             w2_planes[:].rearrange("p t m -> p (t m)"),
             w2_grouped[:].rearrange("p t m j -> p (t m j)"),
         )
         pick_second(0, PACK - 1)
+        for t in range(1):
+            pick_second(1, t)
         z_grouped = {}
         z_codes = {}
         z_planes = {}
         y = {}
 
         def merge(c):
-            z_grouped[c] = keep.tile([P, HALF, PACK], BF16, name="z_grouped", align_bytes=64)
+            z_grouped[c] = keep.tile([P, SPANS[c][1], PACK], BF16, name="z_grouped", align_bytes=64)
             nc.vector.tensor_tensor(
                 z_grouped[c][:].rearrange("p (a i) t -> p a t i", i=4),
                 first[c][:].rearrange("p t (a i) -> p a t i", i=4),
@@ -222,46 +230,46 @@ def tile_picked_zunm_relu_po_kernel(
             )
 
         def quantize_z(c):
-            z_codes[c] = keep.tile([P, HALF], U32, name="z_codes%d" % c, align_bytes=64)
-            z_planes[c] = keep.tile([P, HALF], U8, name="z_planes%d" % c, align_bytes=64)
+            z_codes[c] = keep.tile([P, SPANS[c][1]], U32, name="z_codes%d" % c, align_bytes=64)
+            z_planes[c] = keep.tile([P, SPANS[c][1]], U8, name="z_planes%d" % c, align_bytes=64)
             quantize(z_codes[c][:], z_planes[c][:], z_grouped[c][:].rearrange("p v t -> p (v t)"))
 
-        y_bank = {}
-
-        def second_product(c):
-            for pair in range(2):
-                y_bank[c, pair] = psum.tile([P, 2, HALF], F32, name="y_bank", tag="bank%d" % (2 * c + pair))
-                for s in range(2):
-                    nc.tensor.matmul_mx(
-                        out=y_bank[c, pair][:, s, :],
-                        lhsT=w2_codes[:, 2 * pair + s, :].bitcast(FP8X4),
-                        lhsT_scale=w2_planes[:, 2 * pair + s, :],
-                        rhs=z_codes[c][:].bitcast(FP8X4),
-                        rhs_scale=z_planes[c][:],
-                        start=True,
-                        stop=True,
-                    )
-
-        def unload(c, pair, copy):
-            unloaded = keep.tile([P, 2, HALF], F32, name="y%d_%d" % (c, pair), align_bytes=64)
-            copy(unloaded[:], y_bank[c, pair][:])
-            for s in range(2):
-                y[c, 2 * pair + s] = unloaded[:, s, :]
+        def second_product(target, c, t, cols):
+            nc.tensor.matmul_mx(
+                out=target,
+                lhsT=w2_codes[:, t, :].bitcast(FP8X4),
+                lhsT_scale=w2_planes[:, t, :],
+                rhs=z_codes[c][:, cols].bitcast(FP8X4),
+                rhs_scale=z_planes[c][:, cols],
+                start=True,
+                stop=True,
+            )
 
         merge(0)
         quantize_z(0)
-        pick_second(1, PACK - 1)
-        second_product(0)
-        first.append(after_table0.tile([P, PACK, HALF], F32, name="first1", offset=8192, align_bytes=64))
+        for t in range(1, PACK):
+            pick_second(1, t)
+        back_sb[0] = after_table0.tile([P, EARLY], F32, name="back0", offset=8704, align_bytes=64)
+        nc.sync.dma_start(out=back_sb[0][:], in_=back[:, :EARLY])
+        early_bank = psum.tile([P, PACK, EARLY], F32, name="early_bank", tag="bank0")
+        for t in range(PACK):
+            second_product(early_bank[:, t, :], 0, t, slice(0, EARLY))
+        first.append(after_table0.tile([P, PACK, LATE], F32, name="first1", offset=2560, align_bytes=64))
         for t in range(PACK):
             pick_first(1, t)
-        unload(0, 1, nc.scalar.copy)
-        unload(0, 0, nc.scalar.copy)
+        early_y = keep.tile([P, PACK, EARLY], F32, name="early_y", align_bytes=64)
+        nc.scalar.copy(early_y[:], early_bank[:])
+        for t in range(PACK):
+            y[0, t] = early_y[:, t, :]
         merge(1)
         quantize_z(1)
-        second_product(1)
-        unload(1, 0, nc.scalar.copy)
-        unload(1, 1, nc.vector.tensor_copy)
+        for t in (2, 0, 1, 3):
+            late_bank = psum.tile([P, LATE], F32, name="late_bank", tag="bank%d" % (1 + t))
+            for cols in (slice(0, 256), slice(256, LATE)):
+                second_product(late_bank[:, cols], 1, t, cols)
+            late_y = keep.tile([P, LATE], F32, name="late_y%d" % t, align_bytes=64)
+            (nc.vector.tensor_copy if t in () else nc.scalar.copy)(late_y[:], late_bank[:])
+            y[1, t] = late_y[:]
 
         window = [keep.tile([P, S], F32, name="window%d" % t) for t in range(PACK)]
         out_rows = out_0.rearrange("(p t) c -> p t c", t=PACK)
@@ -269,23 +277,23 @@ def tile_picked_zunm_relu_po_kernel(
         out_grouped = keep.tile([P, S, PACK], BF16, name="out_grouped", align_bytes=64)
 
         def scatter_first(c, t):
-            nc.scalar.activation(window[t][:].indirect(entries(ka_sb, HALF * c, HALF)), y[c, t], COPY)
+            nc.scalar.activation(window[t][:].indirect(entries(ka_sb, *SPANS[c])), y[c, t], COPY)
 
         def scatter_second(c, t):
-            nc.vector.tensor_tensor(
-                window[t][:].indirect(entries(kb_sb, HALF * c, HALF)), y[c, t], back_sb[:, HALF * c : HALF * (c + 1)], MULT
-            )
+            nc.vector.tensor_tensor(window[t][:].indirect(entries(kb_sb, *SPANS[c])), y[c, t], back_sb[c][:], MULT)
 
-        steps = ((0, 0), (0, 1), (0, 3), (1, 0), (1, 1), (1, 2), (1, 3), (0, 2))
-        behind = steps[-1]
-        for step in steps:
-            scatter_first(*step)
-            scatter_second(*behind)
-            if behind in ((1, 0), (1, 1)):
-                done = behind[1]
-                nc.sync.dma_start(out=collected[:, done, :], in_=window[done][:])
-                nc.sync.dma_start(out=out_rows[:, done, :], in_=window[done][:])
-            behind = step
+        for t in range(PACK):
+            scatter_first(0, t)
+        for t in range(PACK):
+            scatter_second(0, t)
+        behind = 2
+        for t in (0, 1, 3, 2):
+            scatter_first(1, t)
+            scatter_second(1, behind)
+            if behind < 2:
+                nc.sync.dma_start(out=collected[:, behind, :], in_=window[behind][:])
+                nc.sync.dma_start(out=out_rows[:, behind, :], in_=window[behind][:])
+            behind = t
         for done in (2, 3):
             nc.sync.dma_start(out=out_rows[:, done, :], in_=window[done][:])
 

@@ -95,14 +95,17 @@ def tile_picked_zunm_relu_po_kernel(
         table.append(shared.tile([P, T], U32, name="table1", offset=0, align_bytes=64))
         load_table(1, 1)
         place_scales(1, range(2, 4))
-        w1_raw.append(after_table0.tile([P, PACK, H], F32, name="w1_raw1", offset=0, align_bytes=64))
+        w1_last = [
+            after_table0.tile([P, PACK, H // 2], F32, name="w1_last%d" % n, offset=4096 * n, align_bytes=64) for n in range(2)
+        ]
         gate_sb = [
             after_table0.tile([P, EARLY], F32, name="gate0", offset=8192, align_bytes=64),
             after_table0.tile([P, LATE], F32, name="gate1", offset=8704, align_bytes=64),
         ]
         back_sb = {1: after_table0.tile([P, LATE], F32, name="back1", offset=13312, align_bytes=64)}
         w2_raw = after_table0.tile([P, PACK, N], F32, name="w2_raw", offset=15360, align_bytes=64)
-        nc.sync.dma_start(out=w1_raw[1][:], in_=w1_rows[1])
+        for n in range(2):
+            nc.sync.dma_start(out=w1_last[n][:], in_=w1_rows[1][:, :, n * H // 2 : (n + 1) * H // 2])
         for c, (start, count) in enumerate(SPANS):
             nc.sync.dma_start(out=gate_sb[c][:], in_=gate[:, start : start + count])
         w2_rows = w2.rearrange("(g j r) c -> j g r c", j=PACK, r=RUN)
@@ -117,15 +120,10 @@ def tile_picked_zunm_relu_po_kernel(
         halves = S // BANK
         acc = {}
 
-        def group_w1(o, t, copy):
-            if o == 0:
-                grouped = keep.tile([P, P, PACK], BF16, name="w1_grouped0_%d" % t, align_bytes=64)
-            else:
-                grouped = shared.tile([P, P, PACK], BF16, name="w1_grouped1_%d" % t, offset=1024 * t, align_bytes=64)
-            w1_grouped[o, t] = grouped
+        def group_w1(grouped, raw, t, copy):
             copy(
-                grouped[:].rearrange("p (g a i) j -> p g a j i", a=2, i=4),
-                w1_raw[o][:].rearrange("p j (g t a i) -> p t g a j i", t=PACK, a=2, i=4)[:, t],
+                grouped.rearrange("p (g a i) j -> p g a j i", a=2, i=4),
+                raw.rearrange("p j (g t a i) -> p t g a j i", t=PACK, a=2, i=4)[:, t],
             )
 
         def quantize_w1(o, t):
@@ -159,23 +157,20 @@ def tile_picked_zunm_relu_po_kernel(
                 nc.scalar.activation(h[t][:, tokens], acc[t, half][:], RELU)
 
         for t in range(PACK):
-            group_w1(0, t, nc.scalar.copy)
+            w1_grouped[0, t] = keep.tile([P, P, PACK], BF16, name="w1_grouped0_%d" % t, align_bytes=64)
+            group_w1(w1_grouped[0, t][:], w1_raw[0][:], t, nc.scalar.copy)
             quantize_w1(0, t)
         for t in range(PACK):
             first_product(0, t)
         x_codes.append(keep.tile([P, S], U32, name="x_codes1", align_bytes=64))
         nc.vector.tensor_copy(x_codes[1][:], table[1][:].indirect(offs_sb[:]))
-        group_w1(1, 0, nc.vector.tensor_copy)
-        group_w1(1, 1, nc.vector.tensor_copy)
-        group_w1(1, 2, nc.scalar.copy)
-        group_w1(1, 3, nc.scalar.copy)
-        quantize_w1(1, 0)
-        quantize_w1(1, 1)
-        first_product(1, 0)
-        first_product(1, 1)
-        quantize_w1(1, 2)
-        quantize_w1(1, 3)
-        for t in range(2, PACK):
+        for t in range(PACK):
+            w1_grouped[1, t] = keep.tile([P, P, PACK], BF16, name="w1_grouped1_%d" % t, align_bytes=64)
+            group_w1(w1_grouped[1, t][:, : P // 2, :], w1_last[0][:], t, nc.scalar.copy)
+        for t in range(PACK):
+            group_w1(w1_grouped[1, t][:, P // 2 :, :], w1_last[1][:], t, nc.vector.tensor_copy if t < 1 else nc.scalar.copy)
+        for t in range(PACK):
+            quantize_w1(1, t)
             first_product(1, t)
 
         first = [keep.tile([P, PACK, EARLY], F32, name="first0", align_bytes=64)]
@@ -192,16 +187,16 @@ def tile_picked_zunm_relu_po_kernel(
         def pick_second(c, t):
             nc.vector.tensor_tensor(second[c][:, t, :], h[t][:].indirect(entries(kb_sb, *SPANS[c])), gate_sb[c][:], MULT)
 
-        w2_grouped = shared.tile([P, PACK, P, PACK], BF16, name="w2_grouped", offset=0, align_bytes=64)
+        w2_grouped = keep.tile([P, PACK, P, PACK], BF16, name="w2_grouped", align_bytes=64)
         w2_codes = keep.tile([P, PACK, P], U32, name="w2_codes", align_bytes=64)
         w2_planes = keep.tile([P, PACK, P], U8, name="w2_planes", align_bytes=64)
 
         for t in range(PACK):
             relu(t, 0, False)
-            relu(t, 1, t in (0,))
+            relu(t, 1, t in (0, 1))
             if t == 1:
                 nc.vector.tensor_copy(
-                    w2_grouped[:].rearrange("p t m j -> p m t j"), w2_raw[:].rearrange("p j (m t) -> p m t j", t=PACK)
+                    w2_grouped[:].rearrange("p t m j -> p m j t"), w2_raw[:].rearrange("p j (m t) -> p m j t", t=PACK)
                 )
         for t in range(PACK):
             pick_first(0, t)

@@ -24,10 +24,16 @@ K_PASS = P * PACK
 BANK = 512
 LIST_ROWS = 16
 PASSES = K // K_PASS
+QUADRANTS = 4
+RUN = 8
+LINE = 4
 EARLY = 128
 LATE = V - EARLY
 SPANS = ((0, EARLY), (EARLY, LATE))
-RUN = 8
+RELU_ON_VECTOR = (0, 1)
+SPLIT = 576
+LAST_PIECE = S - 128
+PIECES = ((0, 256), (256, 512), (512, LAST_PIECE), (LAST_PIECE, S))
 
 
 def tile_picked_zunm_relu_po_kernel(
@@ -52,27 +58,25 @@ def tile_picked_zunm_relu_po_kernel(
         kb_sb = keep.tile([P, V // LIST_ROWS], U16, name="kb_sb")
         table = [after_table0.tile([P, T], U32, name="table0", offset=0, align_bytes=64)]
         table_scales = shared.tile([P, T], U8, name="table_scales", offset=0, align_bytes=64)
-        w1_raw = [keep.tile([P, PACK, H], F32, name="w1_raw0")]
+        w1_first = keep.tile([P, PACK, H], F32, name="w1_raw0")
 
-        def load_table(o, pieces):
+        def load_table(o):
             words = x_words[o].rearrange("p n t -> p (n t)").bitcast(I32)
-            for c in range(pieces):
-                cols = slice(c * T // pieces, (c + 1) * T // pieces)
-                nc.sync.dma_start(out=table[o][:, cols].bitcast(I32), in_=words[:, cols])
+            nc.sync.dma_start(out=table[o][:].bitcast(I32), in_=words)
 
         nc.gpsimd.memset(table_scales[:, : T // 2].bitcast(I32), 0)
         nc.vector.memset(table_scales[:, T // 2 :].bitcast(I32), 0)
         w1_rows = w1.rearrange("(o p j) c -> o p j c", o=PASSES, j=PACK)
-        nc.sync.dma_start(out=w1_raw[0][:, 0, :], in_=w1_rows[0][:, 0, :])
+        nc.sync.dma_start(out=w1_first[:, 0, :], in_=w1_rows[0][:, 0, :])
         nc.sync.dma_start(offs_sb[:], offs)
         nc.sync.dma_start(kb_sb[:], kb)
         nc.sync.dma_start(ka_sb[:], ka)
-        nc.sync.dma_start(out=w1_raw[0][:, 1, :], in_=w1_rows[0][:, 1, :])
+        nc.sync.dma_start(out=w1_first[:, 1, :], in_=w1_rows[0][:, 1, :])
         nc.sync.dma_start(
             out=table_scales[0:P:4, :].bitcast(I32), in_=x_scales.rearrange("o r c -> (o r) c").bitcast(I32)
         )
-        nc.sync.dma_start(out=w1_raw[0][:, 2:, :], in_=w1_rows[0][:, 2:, :])
-        load_table(0, 1)
+        nc.sync.dma_start(out=w1_first[:, 2:, :], in_=w1_rows[0][:, 2:, :])
+        load_table(0)
 
         picked_scales = keep.tile([P, S], U8, name="picked_scales", align_bytes=64)
         x_planes = [keep.tile([P, S], U8, name="x_planes%d" % o, align_bytes=64) for o in range(PASSES)]
@@ -90,17 +94,19 @@ def tile_picked_zunm_relu_po_kernel(
                     in_=picked_scales[source : source + 16 : 4, :].bitcast(I32),
                 )
 
-        place_scales(0, range(4))
+        place_scales(0, range(QUADRANTS))
         place_scales(1, range(2))
         table.append(shared.tile([P, T], U32, name="table1", offset=0, align_bytes=64))
-        load_table(1, 1)
-        place_scales(1, range(2, 4))
+        load_table(1)
+        place_scales(1, range(2, QUADRANTS))
+
         w1_last = [
             after_table0.tile([P, PACK, H // 2], F32, name="w1_last%d" % n, offset=4096 * n, align_bytes=64) for n in range(2)
         ]
+        gate_offset = (8192, 8192 + 4 * EARLY)
         gate_sb = [
-            after_table0.tile([P, EARLY], F32, name="gate0", offset=8192, align_bytes=64),
-            after_table0.tile([P, LATE], F32, name="gate1", offset=8704, align_bytes=64),
+            after_table0.tile([P, EARLY], F32, name="gate0", offset=gate_offset[0], align_bytes=64),
+            after_table0.tile([P, LATE], F32, name="gate1", offset=gate_offset[1], align_bytes=64),
         ]
         back_sb = {1: after_table0.tile([P, LATE], F32, name="back1", offset=13312, align_bytes=64)}
         w2_raw = after_table0.tile([P, PACK, N], F32, name="w2_raw", offset=15360, align_bytes=64)
@@ -122,8 +128,8 @@ def tile_picked_zunm_relu_po_kernel(
 
         def group_w1(grouped, raw, t, copy):
             copy(
-                grouped.rearrange("p (g a i) j -> p g a j i", a=2, i=4),
-                raw.rearrange("p j (g t a i) -> p t g a j i", t=PACK, a=2, i=4)[:, t],
+                grouped.rearrange("p (g a i) j -> p g a j i", a=RUN // LINE, i=LINE),
+                raw.rearrange("p j (g t a i) -> p t g a j i", t=PACK, a=RUN // LINE, i=LINE)[:, t],
             )
 
         def quantize_w1(o, t):
@@ -158,7 +164,7 @@ def tile_picked_zunm_relu_po_kernel(
 
         for t in range(PACK):
             w1_grouped[0, t] = keep.tile([P, P, PACK], BF16, name="w1_grouped0_%d" % t, align_bytes=64)
-            group_w1(w1_grouped[0, t][:], w1_raw[0][:], t, nc.scalar.copy)
+            group_w1(w1_grouped[0, t][:], w1_first[:], t, nc.scalar.copy)
             quantize_w1(0, t)
         for t in range(PACK):
             first_product(0, t)
@@ -168,7 +174,7 @@ def tile_picked_zunm_relu_po_kernel(
             w1_grouped[1, t] = keep.tile([P, P, PACK], BF16, name="w1_grouped1_%d" % t, align_bytes=64)
             group_w1(w1_grouped[1, t][:, : P // 2, :], w1_last[0][:], t, nc.scalar.copy)
         for t in range(PACK):
-            group_w1(w1_grouped[1, t][:, P // 2 :, :], w1_last[1][:], t, nc.vector.tensor_copy if t < 1 else nc.scalar.copy)
+            group_w1(w1_grouped[1, t][:, P // 2 :, :], w1_last[1][:], t, nc.vector.tensor_copy if t == 0 else nc.scalar.copy)
         for t in range(PACK):
             quantize_w1(1, t)
             first_product(1, t)
@@ -193,8 +199,8 @@ def tile_picked_zunm_relu_po_kernel(
 
         for t in range(PACK):
             relu(t, 0, False)
-            relu(t, 1, t in (0, 1))
-            if t == 1:
+            relu(t, 1, t in RELU_ON_VECTOR)
+            if t == RELU_ON_VECTOR[-1]:
                 nc.vector.tensor_copy(
                     w2_grouped[:].rearrange("p t m j -> p m j t"), w2_raw[:].rearrange("p j (m t) -> p m j t", t=PACK)
                 )
@@ -208,8 +214,7 @@ def tile_picked_zunm_relu_po_kernel(
             w2_grouped[:].rearrange("p t m j -> p (t m j)"),
         )
         pick_second(0, PACK - 1)
-        for t in range(1):
-            pick_second(1, t)
+        pick_second(1, 0)
         z_grouped = {}
         z_codes = {}
         z_planes = {}
@@ -218,9 +223,9 @@ def tile_picked_zunm_relu_po_kernel(
         def merge(c):
             z_grouped[c] = keep.tile([P, SPANS[c][1], PACK], BF16, name="z_grouped", align_bytes=64)
             nc.vector.tensor_tensor(
-                z_grouped[c][:].rearrange("p (a i) t -> p a t i", i=4),
-                first[c][:].rearrange("p t (a i) -> p a t i", i=4),
-                second[c].rearrange("p t (a i) -> p a t i", i=4),
+                z_grouped[c][:].rearrange("p (a i) t -> p a t i", i=LINE),
+                first[c][:].rearrange("p t (a i) -> p a t i", i=LINE),
+                second[c].rearrange("p t (a i) -> p a t i", i=LINE),
                 ADD,
             )
 
@@ -244,12 +249,13 @@ def tile_picked_zunm_relu_po_kernel(
         quantize_z(0)
         for t in range(1, PACK):
             pick_second(1, t)
-        back_sb[0] = after_table0.tile([P, EARLY], F32, name="back0", offset=8704, align_bytes=64)
+        back_sb[0] = after_table0.tile([P, EARLY], F32, name="back0", offset=gate_offset[1], align_bytes=64)
         nc.sync.dma_start(out=back_sb[0][:], in_=back[:, :EARLY])
         early_bank = psum.tile([P, PACK, EARLY], F32, name="early_bank", tag="bank0")
         for t in range(PACK):
             second_product(early_bank[:, t, :], 0, t, slice(0, EARLY))
-        first.append(after_table0.tile([P, PACK, LATE], F32, name="first1", offset=2560, align_bytes=64))
+        first_offset = gate_offset[1] - 4 * PACK * LATE
+        first.append(after_table0.tile([P, PACK, LATE], F32, name="first1", offset=first_offset, align_bytes=64))
         for t in range(PACK):
             pick_first(1, t)
         early_y = keep.tile([P, PACK, EARLY], F32, name="early_y", align_bytes=64)
@@ -258,12 +264,14 @@ def tile_picked_zunm_relu_po_kernel(
             y[0, t] = early_y[:, t, :]
         merge(1)
         quantize_z(1)
-        for t in (2, 0, 1, 3):
+        late_order = (0, 1, 3, 2)
+        vector_order = late_order[-1:] + late_order[:-1]
+        for t in vector_order:
             late_bank = psum.tile([P, LATE], F32, name="late_bank", tag="bank%d" % (1 + t))
             for cols in (slice(0, 256), slice(256, LATE)):
                 second_product(late_bank[:, cols], 1, t, cols)
             late_y = keep.tile([P, LATE], F32, name="late_y%d" % t, align_bytes=64)
-            (nc.vector.tensor_copy if t in () else nc.scalar.copy)(late_y[:], late_bank[:])
+            nc.scalar.copy(late_y[:], late_bank[:])
             y[1, t] = late_y[:]
 
         window = [keep.tile([P, S], F32, name="window%d" % t) for t in range(PACK)]
@@ -281,39 +289,39 @@ def tile_picked_zunm_relu_po_kernel(
             scatter_first(0, t)
         for t in range(PACK):
             scatter_second(0, t)
-        behind = 2
-        for t in (0, 1, 3, 2):
-            scatter_first(1, t)
-            scatter_second(1, behind)
-            if behind < 2:
-                nc.sync.dma_start(out=collected[:, behind, :], in_=window[behind][:])
-                nc.sync.dma_start(out=out_rows[:, behind, :], in_=window[behind][:])
-            behind = t
-        for done in (2, 3):
-            nc.sync.dma_start(out=out_rows[:, done, :], in_=window[done][:])
+        last_tiles = (2, 3)
+        for scalar_tile, vector_tile in zip(late_order, vector_order):
+            scatter_first(1, scalar_tile)
+            scatter_second(1, vector_tile)
+            if vector_tile not in last_tiles:
+                nc.sync.dma_start(out=collected[:, vector_tile, :], in_=window[vector_tile][:])
+                nc.sync.dma_start(out=out_rows[:, vector_tile, :], in_=window[vector_tile][:])
+        for t in last_tiles:
+            nc.sync.dma_start(out=out_rows[:, t, :], in_=window[t][:])
 
         out_codes = keep.tile([P, S], U32, name="out_codes", align_bytes=64)
         out_planes = keep.tile([P, S], U8, name="out_planes", align_bytes=64)
         words_out = out_1[0].rearrange("p n t -> p (n t)").bitcast(I32)
-        split = 576
-        for start, stop, copy in ((0, split, nc.vector.tensor_copy), (split, S, nc.scalar.copy)):
-            for done in (2, 3):
-                copy(collected[:, done, start:stop], window[done][:, start:stop])
+        for start, stop, copy in ((0, SPLIT, nc.vector.tensor_copy), (SPLIT, S, nc.scalar.copy)):
+            for t in last_tiles:
+                copy(collected[:, t, start:stop], window[t][:, start:stop])
         for start, stop, copy in (
-            (0, 256, nc.vector.tensor_copy),
-            (split, 896, nc.scalar.copy),
-            (256, split, nc.vector.tensor_copy),
-            (896, S, nc.scalar.copy),
+            (0, PIECES[0][1], nc.vector.tensor_copy),
+            (SPLIT, LAST_PIECE, nc.scalar.copy),
+            (PIECES[0][1], SPLIT, nc.vector.tensor_copy),
+            (LAST_PIECE, S, nc.scalar.copy),
         ):
             copy(
-                out_grouped[:, start:stop, :].rearrange("p (a i) t -> p a t i", i=4),
-                collected[:, :, start:stop].rearrange("p t (a i) -> p a t i", i=4),
+                out_grouped[:, start:stop, :].rearrange("p (a i) t -> p a t i", i=LINE),
+                collected[:, :, start:stop].rearrange("p t (a i) -> p a t i", i=LINE),
             )
-        for start, stop in ((0, 256), (256, 512), (512, 896), (896, S)):
+        for start, stop in PIECES:
             cols = slice(start, stop)
             quantize(out_codes[:, cols], out_planes[:, cols], out_grouped[:, cols, :].rearrange("p c t -> p (c t)"))
-            nc.sync.dma_start(out=words_out[:, cols], in_=out_codes[:, cols].bitcast(I32))
-        for q in range(4):
+            if start > 0:
+                stored = slice(0 if start == PIECES[1][0] else start, stop)
+                nc.sync.dma_start(out=words_out[:, stored], in_=out_codes[:, stored].bitcast(I32))
+        for q in range(QUADRANTS):
             queue = nc.scalar if q % 2 else nc.sync
             queue.dma_start(
                 out=out_2[0, 4 * q : 4 * q + 4, :].bitcast(I32),

@@ -30,6 +30,7 @@ LINE = 4
 EARLY = 128
 LATE = V - EARLY
 SPANS = ((0, EARLY), (EARLY, LATE))
+Z_PIECES = ((slice(0, 64), slice(64, EARLY)), (slice(0, 256), slice(256, LATE)))
 RELU_ON_VECTOR = (0, 1)
 SPLIT = 576
 LAST_PIECE = S - 128
@@ -190,8 +191,10 @@ def tile_picked_zunm_relu_po_kernel(
         def pick_first(c, t):
             nc.scalar.activation(first[c][:, t, :], h[t][:].indirect(entries(ka_sb, *SPANS[c])), COPY)
 
-        def pick_second(c, t):
-            nc.vector.tensor_tensor(second[c][:, t, :], h[t][:].indirect(entries(kb_sb, *SPANS[c])), gate_sb[c][:], MULT)
+        def pick_second(c, t, cols=None):
+            cols = cols or slice(0, SPANS[c][1])
+            picked = h[t][:].indirect(entries(kb_sb, SPANS[c][0] + cols.start, cols.stop - cols.start))
+            nc.vector.tensor_tensor(second[c][:, t, cols], picked, gate_sb[c][:, cols], MULT)
 
         w2_grouped = keep.tile([P, PACK, P, PACK], BF16, name="w2_grouped", align_bytes=64)
         w2_codes = keep.tile([P, PACK, P], U32, name="w2_codes", align_bytes=64)
@@ -222,17 +225,19 @@ def tile_picked_zunm_relu_po_kernel(
 
         def merge(c):
             z_grouped[c] = keep.tile([P, SPANS[c][1], PACK], BF16, name="z_grouped", align_bytes=64)
-            nc.vector.tensor_tensor(
-                z_grouped[c][:].rearrange("p (a i) t -> p a t i", i=LINE),
-                first[c][:].rearrange("p t (a i) -> p a t i", i=LINE),
-                second[c].rearrange("p t (a i) -> p a t i", i=LINE),
-                ADD,
-            )
+            for cols in Z_PIECES[c]:
+                nc.vector.tensor_tensor(
+                    z_grouped[c][:, cols, :].rearrange("p (a i) t -> p a t i", i=LINE),
+                    first[c][:, :, cols].rearrange("p t (a i) -> p a t i", i=LINE),
+                    second[c][:, :, cols].rearrange("p t (a i) -> p a t i", i=LINE),
+                    ADD,
+                )
 
         def quantize_z(c):
             z_codes[c] = keep.tile([P, SPANS[c][1]], U32, name="z_codes%d" % c, align_bytes=64)
             z_planes[c] = keep.tile([P, SPANS[c][1]], U8, name="z_planes%d" % c, align_bytes=64)
-            quantize(z_codes[c][:], z_planes[c][:], z_grouped[c][:].rearrange("p v t -> p (v t)"))
+            for cols in Z_PIECES[c]:
+                quantize(z_codes[c][:, cols], z_planes[c][:, cols], z_grouped[c][:, cols, :].rearrange("p v t -> p (v t)"))
 
         def second_product(target, c, t, cols):
             nc.tensor.matmul_mx(
@@ -247,8 +252,10 @@ def tile_picked_zunm_relu_po_kernel(
 
         merge(0)
         quantize_z(0)
-        for t in range(1, PACK):
+        for t in range(1, PACK - 1):
             pick_second(1, t)
+        for cols in Z_PIECES[1]:
+            pick_second(1, PACK - 1, cols)
         back_sb[0] = after_table0.tile([P, EARLY], F32, name="back0", offset=gate_offset[1], align_bytes=64)
         nc.sync.dma_start(out=back_sb[0][:], in_=back[:, :EARLY])
         early_bank = psum.tile([P, PACK, EARLY], F32, name="early_bank", tag="bank0")
@@ -256,10 +263,11 @@ def tile_picked_zunm_relu_po_kernel(
             second_product(early_bank[:, t, :], 0, t, slice(0, EARLY))
         first_offset = gate_offset[1] - 4 * PACK * LATE
         first.append(after_table0.tile([P, PACK, LATE], F32, name="first1", offset=first_offset, align_bytes=64))
-        for t in range(PACK):
+        for t in range(PACK - 1):
             pick_first(1, t)
         early_y = keep.tile([P, PACK, EARLY], F32, name="early_y", align_bytes=64)
         nc.scalar.copy(early_y[:], early_bank[:])
+        pick_first(1, PACK - 1)
         for t in range(PACK):
             y[0, t] = early_y[:, t, :]
         merge(1)
@@ -302,9 +310,13 @@ def tile_picked_zunm_relu_po_kernel(
         out_codes = keep.tile([P, S], U32, name="out_codes", align_bytes=64)
         out_planes = keep.tile([P, S], U8, name="out_planes", align_bytes=64)
         words_out = out_1[0].rearrange("p n t -> p (n t)").bitcast(I32)
-        for start, stop, copy in ((0, SPLIT, nc.vector.tensor_copy), (SPLIT, S, nc.scalar.copy)):
-            for t in last_tiles:
-                copy(collected[:, t, start:stop], window[t][:, start:stop])
+        for start, cut, stop, copy, tiles in (
+            (0, PIECES[0][1], SPLIT, nc.vector.tensor_copy, last_tiles),
+            (SPLIT, LAST_PIECE, S, nc.scalar.copy, last_tiles[::-1]),
+        ):
+            copy(collected[:, tiles[0], start:stop], window[tiles[0]][:, start:stop])
+            copy(collected[:, tiles[1], start:cut], window[tiles[1]][:, start:cut])
+            copy(collected[:, tiles[1], cut:stop], window[tiles[1]][:, cut:stop])
         for start, stop, copy in (
             (0, PIECES[0][1], nc.vector.tensor_copy),
             (SPLIT, LAST_PIECE, nc.scalar.copy),

@@ -46,6 +46,7 @@ def tile_picked_zunm_relu_po_kernel(
         keep = ctx.enter_context(tc.tile_pool(name="keep", bufs=1))
         shared = ctx.enter_context(tc.tile_pool(name="shared", bufs=1))
         after_table0 = ctx.enter_context(tc.tile_pool(name="after_table0", bufs=1))
+        after_h1 = ctx.enter_context(tc.tile_pool(name="after_h1", bufs=1))
         psum = ctx.enter_context(tc.psum_pool(name="psum", bufs=1))
 
         def entries(list_tile, start, count):
@@ -109,7 +110,7 @@ def tile_picked_zunm_relu_po_kernel(
             after_table0.tile([P, EARLY], F32, name="gate0", offset=gate_offset[0], align_bytes=64),
             after_table0.tile([P, LATE], F32, name="gate1", offset=gate_offset[1], align_bytes=64),
         ]
-        back_sb = {1: after_table0.tile([P, LATE], F32, name="back1", offset=13312, align_bytes=64)}
+        late_back = after_table0.tile([P, LATE], F32, name="late_back", offset=13312, align_bytes=64)
         w2_raw = after_table0.tile([P, PACK, N], F32, name="w2_raw", offset=15360, align_bytes=64)
         for n in range(2):
             nc.sync.dma_start(out=w1_last[n][:], in_=w1_rows[1][:, :, n * H // 2 : (n + 1) * H // 2])
@@ -118,7 +119,7 @@ def tile_picked_zunm_relu_po_kernel(
         w2_rows = w2.rearrange("(g j r) c -> j g r c", j=PACK, r=RUN)
         for j in range(PACK):
             nc.sync.dma_start(out=w2_raw[:, j, :], in_=w2_rows[j])
-        nc.sync.dma_start(out=back_sb[1][:], in_=back[:, EARLY:])
+        nc.sync.dma_start(out=late_back[:], in_=back[:, EARLY:])
 
         w1_grouped = {}
         w1_codes = {}
@@ -157,8 +158,12 @@ def tile_picked_zunm_relu_po_kernel(
         def relu(t, half, on_vector):
             tokens = slice(BANK * half, BANK * (half + 1))
             if half == 0:
-                h[t] = keep.tile([P, S], F32, name="h%d" % t)
-            if on_vector:
+                h[t] = after_h1.tile([P, S], F32, name="h1", offset=0) if t == 1 else keep.tile([P, S], F32, name="h%d" % t)
+            if on_vector and t == RELU_ON_VECTOR[-1]:
+                cut = BANK * half + BANK // 2
+                nc.vector.tensor_scalar(h[t][:, tokens.start : cut], acc[t, half][:, : BANK // 2], 0.0, None, MAX)
+                nc.scalar.activation(h[t][:, cut : tokens.stop], acc[t, half][:, BANK // 2 :], RELU)
+            elif on_vector:
                 nc.vector.tensor_scalar(h[t][:, tokens], acc[t, half][:], 0.0, None, MAX)
             else:
                 nc.scalar.activation(h[t][:, tokens], acc[t, half][:], RELU)
@@ -256,8 +261,6 @@ def tile_picked_zunm_relu_po_kernel(
             pick_second(1, t)
         for cols in Z_PIECES[1]:
             pick_second(1, PACK - 1, cols)
-        back_sb[0] = after_table0.tile([P, EARLY], F32, name="back0", offset=gate_offset[1], align_bytes=64)
-        nc.sync.dma_start(out=back_sb[0][:], in_=back[:, :EARLY])
         early_bank = psum.tile([P, PACK, EARLY], F32, name="early_bank", tag="bank0")
         for t in range(PACK):
             second_product(early_bank[:, t, :], 0, t, slice(0, EARLY))
@@ -265,6 +268,9 @@ def tile_picked_zunm_relu_po_kernel(
         first.append(after_table0.tile([P, PACK, LATE], F32, name="first1", offset=first_offset, align_bytes=64))
         for t in range(PACK - 1):
             pick_first(1, t)
+        early_back_sb = after_h1.tile([P, EARLY], F32, name="early_back", offset=0)
+        early_back = early_back_sb[:]
+        nc.sync.dma_start(out=early_back, in_=back[:, :EARLY])
         early_y = keep.tile([P, PACK, EARLY], F32, name="early_y", align_bytes=64)
         nc.scalar.copy(early_y[:], early_bank[:])
         pick_first(1, PACK - 1)
@@ -291,7 +297,7 @@ def tile_picked_zunm_relu_po_kernel(
             nc.scalar.activation(window[t][:].indirect(entries(ka_sb, *SPANS[c])), y[c, t], COPY)
 
         def scatter_second(c, t):
-            nc.vector.tensor_tensor(window[t][:].indirect(entries(kb_sb, *SPANS[c])), y[c, t], back_sb[c][:], MULT)
+            nc.vector.tensor_tensor(window[t][:].indirect(entries(kb_sb, *SPANS[c])), y[c, t], (early_back, late_back[:])[c], MULT)
 
         for t in range(PACK):
             scatter_first(0, t)

@@ -273,7 +273,12 @@ def tile_picked_zunm_relu_po_kernel(
         nc.sync.dma_start(out=early_back, in_=back[:, :EARLY])
         early_y = keep.tile([P, PACK, EARLY], F32, name="early_y", align_bytes=64)
         nc.scalar.copy(early_y[:], early_bank[:])
-        pick_first(1, PACK - 1)
+        wide, narrow = Z_PIECES[1]
+        last_hidden = h[PACK - 1][:]
+        nc.scalar.activation(first[1][:, PACK - 1, wide], last_hidden.indirect(entries(ka_sb, EARLY, wide.stop)), COPY)
+        nc.vector.tensor_copy(
+            first[1][:, PACK - 1, narrow], last_hidden.indirect(entries(ka_sb, EARLY + narrow.start, LATE - narrow.start))
+        )
         for t in range(PACK):
             y[0, t] = early_y[:, t, :]
         merge(1)

@@ -47,6 +47,7 @@ def tile_picked_zunm_relu_po_kernel(
         shared = ctx.enter_context(tc.tile_pool(name="shared", bufs=1))
         after_table0 = ctx.enter_context(tc.tile_pool(name="after_table0", bufs=1))
         after_h1 = ctx.enter_context(tc.tile_pool(name="after_h1", bufs=1))
+        after_w1 = ctx.enter_context(tc.tile_pool(name="after_w1", bufs=1))
         psum = ctx.enter_context(tc.psum_pool(name="psum", bufs=1))
 
         def entries(list_tile, start, count):
@@ -60,7 +61,7 @@ def tile_picked_zunm_relu_po_kernel(
         kb_sb = keep.tile([P, V // LIST_ROWS], U16, name="kb_sb")
         table = [after_table0.tile([P, T], U32, name="table0", offset=0, align_bytes=64)]
         table_scales = shared.tile([P, T], U8, name="table_scales", offset=0, align_bytes=64)
-        w1_first = keep.tile([P, PACK, H], F32, name="w1_raw0")
+        w1_first = after_w1.tile([P, PACK, H], F32, name="w1_raw0", offset=0, align_bytes=64)
 
         def load_table(o):
             words = x_words[o].rearrange("p n t -> p (n t)").bitcast(I32)
@@ -81,26 +82,23 @@ def tile_picked_zunm_relu_po_kernel(
         load_table(0)
 
         picked_scales = keep.tile([P, S], U8, name="picked_scales", align_bytes=64)
-        x_planes = [keep.tile([P, S], U8, name="x_planes%d" % o, align_bytes=64) for o in range(PASSES)]
-        for o in range(PASSES):
-            nc.vector.memset(x_planes[o][:].bitcast(I32), 0)
+        x_planes = [keep.tile([P, S], U8, name="x_planes0", align_bytes=64)]
+        nc.vector.memset(x_planes[0][:].bitcast(I32), 0)
         nc.vector.tensor_copy(picked_scales[:], table_scales[:].indirect(offs_sb[:]))
         x_codes = [keep.tile([P, S], U32, name="x_codes0", align_bytes=64)]
         nc.vector.tensor_copy(x_codes[0][:], table[0][:].indirect(offs_sb[:]))
 
-        def place_scales(o, quadrants):
-            for q in quadrants:
+        def place_scales(o, queue):
+            for q in range(QUADRANTS):
                 source = 64 * o + 16 * q
-                nc.sync.dma_start(
+                queue.dma_start(
                     out=x_planes[o][32 * q + 4 * o : 32 * q + 4 * o + 4, :].bitcast(I32),
                     in_=picked_scales[source : source + 16 : 4, :].bitcast(I32),
                 )
 
-        place_scales(0, range(QUADRANTS))
-        place_scales(1, range(2))
+        place_scales(0, nc.sync)
         table.append(shared.tile([P, T], U32, name="table1", offset=0, align_bytes=64))
         load_table(1)
-        place_scales(1, range(2, QUADRANTS))
 
         w1_last = [
             after_table0.tile([P, PACK, H // 2], F32, name="w1_last%d" % n, offset=4096 * n, align_bytes=64) for n in range(2)
@@ -172,6 +170,9 @@ def tile_picked_zunm_relu_po_kernel(
             w1_grouped[0, t] = keep.tile([P, P, PACK], BF16, name="w1_grouped0_%d" % t, align_bytes=64)
             group_w1(w1_grouped[0, t][:], w1_first[:], t, nc.scalar.copy)
             quantize_w1(0, t)
+        x_planes.append(after_w1.tile([P, S], U8, name="x_planes1", offset=0, align_bytes=64))
+        nc.vector.memset(x_planes[1][:].bitcast(I32), 0)
+        place_scales(1, nc.scalar)
         for t in range(PACK):
             first_product(0, t)
         x_codes.append(keep.tile([P, S], U32, name="x_codes1", align_bytes=64))

@@ -32,7 +32,7 @@ LATE = V - EARLY
 SPANS = ((0, EARLY), (EARLY, LATE))
 Z_PIECES = ((slice(0, 64), slice(64, EARLY)), (slice(0, 256), slice(256, LATE)))
 RELU_ON_VECTOR = (0, 1)
-SPLIT = 576
+SPLIT = 544
 LAST_PIECE = S - 128
 PIECES = ((0, 256), (256, 512), (512, LAST_PIECE), (LAST_PIECE, S))
 
@@ -286,18 +286,23 @@ def tile_picked_zunm_relu_po_kernel(
         quantize_z(1)
         late_order = (0, 1, 3, 2)
         vector_order = late_order[-1:] + late_order[:-1]
-        for t in vector_order:
+        for t in (0, 2, 1, 3):
             late_bank = psum.tile([P, LATE], F32, name="late_bank", tag="bank%d" % (1 + t))
             for cols in (slice(0, 256), slice(256, LATE)):
                 second_product(late_bank[:, cols], 1, t, cols)
             late_y = keep.tile([P, LATE], F32, name="late_y%d" % t, align_bytes=64)
             nc.scalar.copy(late_y[:], late_bank[:])
             y[1, t] = late_y[:]
+        y_back = {}
+        for t in late_order:
+            y_back[t] = keep.tile([P, LATE], F32, name="y_back%d" % t, align_bytes=64)
+            nc.gpsimd.tensor_tensor(y_back[t][:], y[1, t], late_back[:], MULT)
 
         window = [keep.tile([P, S], F32, name="window%d" % t) for t in range(PACK)]
         out_rows = out_0.rearrange("(p t) c -> p t c", t=PACK)
-        collected = keep.tile([P, PACK, S], F32, name="collected", align_bytes=64)
-        out_grouped = keep.tile([P, S, PACK], BF16, name="out_grouped", align_bytes=64)
+        shares = ((0, SPLIT), (SPLIT, S))
+        pairs = [keep.tile([P, 2, stop - start, 2], BF16, name="pairs%d" % start, align_bytes=64) for start, stop in shares]
+        out_grouped = [keep.tile([P, stop - start, PACK], BF16, name="out_grouped%d" % start, align_bytes=64) for start, stop in PIECES]
 
         def scatter_first(c, t):
             nc.scalar.activation(window[t][:].indirect(entries(ka_sb, *SPANS[c])), y[c, t], COPY)
@@ -311,37 +316,42 @@ def tile_picked_zunm_relu_po_kernel(
             scatter_second(0, t)
         last_tiles = (2, 3)
         for scalar_tile, vector_tile in zip(late_order, vector_order):
-            scatter_first(1, scalar_tile)
-            scatter_second(1, vector_tile)
+            nc.scalar.activation(window[scalar_tile][:].indirect(entries(kb_sb, *SPANS[1])), y_back[scalar_tile][:], COPY)
+            nc.vector.tensor_copy(window[vector_tile][:].indirect(entries(ka_sb, *SPANS[1])), y[1, vector_tile])
             if vector_tile not in last_tiles:
-                nc.sync.dma_start(out=collected[:, vector_tile, :], in_=window[vector_tile][:])
                 nc.sync.dma_start(out=out_rows[:, vector_tile, :], in_=window[vector_tile][:])
+                for n, (start, stop) in enumerate(shares):
+                    nc.gpsimd.tensor_scalar(pairs[n][:, 0, :, vector_tile], window[vector_tile][:, start:stop], 1.0, 1.0, MULT, MULT)
         for t in last_tiles:
             nc.sync.dma_start(out=out_rows[:, t, :], in_=window[t][:])
 
         out_codes = keep.tile([P, S], U32, name="out_codes", align_bytes=64)
         out_planes = keep.tile([P, S], U8, name="out_planes", align_bytes=64)
         words_out = out_1[0].rearrange("p n t -> p (n t)").bitcast(I32)
-        for start, cut, stop, copy, tiles in (
-            (0, PIECES[0][1], SPLIT, nc.vector.tensor_copy, last_tiles),
-            (SPLIT, LAST_PIECE, S, nc.scalar.copy, last_tiles[::-1]),
-        ):
-            copy(collected[:, tiles[0], start:stop], window[tiles[0]][:, start:stop])
-            copy(collected[:, tiles[1], start:cut], window[tiles[1]][:, start:cut])
-            copy(collected[:, tiles[1], cut:stop], window[tiles[1]][:, cut:stop])
-        for start, stop, copy in (
-            (0, PIECES[0][1], nc.vector.tensor_copy),
-            (SPLIT, LAST_PIECE, nc.scalar.copy),
-            (PIECES[0][1], SPLIT, nc.vector.tensor_copy),
-            (LAST_PIECE, S, nc.scalar.copy),
-        ):
-            copy(
-                out_grouped[:, start:stop, :].rearrange("p (a i) t -> p a t i", i=LINE),
-                collected[:, :, start:stop].rearrange("p t (a i) -> p a t i", i=LINE),
-            )
-        for start, stop in PIECES:
+        def round_pairs(n, start, stop, copy):
+            first_col = shares[n][0]
+            for t in last_tiles:
+                copy(pairs[n][:, 1, start - first_col : stop - first_col, t - 2], window[t][:, start:stop])
+
+        def weave(n, start, stop, copy, dtype):
+            piece = max(k for k in range(len(PIECES)) if PIECES[k][0] <= start)
+            count = stop - start
+            target = out_grouped[piece][:].rearrange("p c t -> p (c t)").bitcast(dtype).rearrange("p (c u) -> p c u", u=2)
+            source = pairs[n][:].rearrange("p u c e -> p u (c e)").bitcast(dtype).rearrange("p u c -> p c u")
+            at, first_col = start - PIECES[piece][0], start - shares[n][0]
+            copy(target[:, at : at + count, :], source[:, first_col : first_col + count, :])
+
+        round_pairs(0, 0, 256, nc.vector.tensor_copy)
+        round_pairs(0, 256, SPLIT, nc.vector.tensor_copy)
+        round_pairs(1, SPLIT, LAST_PIECE, nc.scalar.copy)
+        round_pairs(1, LAST_PIECE, S, nc.scalar.copy)
+        for start, stop in ((0, 256), (256, 512), (512, SPLIT)):
+            weave(0, start, stop, nc.vector.tensor_copy, I32)
+        for start, stop in ((SPLIT, LAST_PIECE), (LAST_PIECE, S)):
+            weave(1, start, stop, nc.scalar.copy, U32)
+        for piece, (start, stop) in enumerate(PIECES):
             cols = slice(start, stop)
-            quantize(out_codes[:, cols], out_planes[:, cols], out_grouped[:, cols, :].rearrange("p c t -> p (c t)"))
+            quantize(out_codes[:, cols], out_planes[:, cols], out_grouped[piece][:].rearrange("p c t -> p (c t)"))
             if start > 0:
                 stored = slice(0 if start == PIECES[1][0] else start, stop)
                 nc.sync.dma_start(out=words_out[:, stored], in_=out_codes[:, stored].bitcast(I32))

@@ -286,7 +286,7 @@ def tile_picked_zunm_relu_po_kernel(
         quantize_z(1)
         late_order = (0, 1, 3, 2)
         vector_order = late_order[-1:] + late_order[:-1]
-        for t in (0, 2, 1, 3):
+        for t in vector_order:
             late_bank = psum.tile([P, LATE], F32, name="late_bank", tag="bank%d" % (1 + t))
             for cols in (slice(0, 256), slice(256, LATE)):
                 second_product(late_bank[:, cols], 1, t, cols)
@@ -294,7 +294,7 @@ def tile_picked_zunm_relu_po_kernel(
             nc.scalar.copy(late_y[:], late_bank[:])
             y[1, t] = late_y[:]
         y_back = {}
-        for t in late_order:
+        for t in (1, 0, 3, 2):
             y_back[t] = keep.tile([P, LATE], F32, name="y_back%d" % t, align_bytes=64)
             nc.gpsimd.tensor_tensor(y_back[t][:], y[1, t], late_back[:], MULT)
 
@@ -316,8 +316,12 @@ def tile_picked_zunm_relu_po_kernel(
             scatter_second(0, t)
         last_tiles = (2, 3)
         for scalar_tile, vector_tile in zip(late_order, vector_order):
-            nc.scalar.activation(window[scalar_tile][:].indirect(entries(kb_sb, *SPANS[1])), y_back[scalar_tile][:], COPY)
-            nc.vector.tensor_copy(window[vector_tile][:].indirect(entries(ka_sb, *SPANS[1])), y[1, vector_tile])
+            sides = ((ka_sb, y[1, scalar_tile]), (kb_sb, y_back[scalar_tile][:]))
+            list_tile, values = sides[scalar_tile != 0]
+            nc.scalar.activation(window[scalar_tile][:].indirect(entries(list_tile, *SPANS[1])), values, COPY)
+            sides = ((ka_sb, y[1, vector_tile]), (kb_sb, y_back[vector_tile][:]))
+            list_tile, values = sides[vector_tile == 0]
+            nc.vector.tensor_copy(window[vector_tile][:].indirect(entries(list_tile, *SPANS[1])), values)
             if vector_tile not in last_tiles:
                 nc.sync.dma_start(out=out_rows[:, vector_tile, :], in_=window[vector_tile][:])
                 for n, (start, stop) in enumerate(shares):

from contextlib import ExitStack

import concourse.mybir as mybir

K, T, S, H, N, V = 1024, 4096, 1024, 512, 512, 512
FLOPS = 2 * K * H * S + 2 * H * N * V

F32 = mybir.dt.float32
BF16 = mybir.dt.bfloat16
I32 = mybir.dt.int32
U32 = mybir.dt.uint32
U16 = mybir.dt.uint16
U8 = mybir.dt.uint8
FP8X4 = mybir.dt.float8_e4m3fn_x4
ADD = mybir.AluOpType.add
MAX = mybir.AluOpType.max
MULT = mybir.AluOpType.mult
RELU = mybir.ActivationFunctionType.Relu
COPY = mybir.ActivationFunctionType.Copy

P = 128
PACK = 4
K_PASS = P * PACK
BANK = 512
LIST_ROWS = 16
PASSES = K // K_PASS
QUADRANTS = 4
RUN = 8
LINE = 4
EARLY = 128
LATE = V - EARLY
SPANS = ((0, EARLY), (EARLY, LATE))
Z_PIECES = ((slice(0, 64), slice(64, EARLY)), (slice(0, 256), slice(256, LATE)))
RELU_ON_VECTOR = (0, 1)
SPLIT = 544
LAST_PIECE = S - 128
PIECES = ((0, 256), (256, 512), (512, LAST_PIECE), (LAST_PIECE, S))


def tile_picked_zunm_relu_po_kernel(
    tc, x_words, x_scales, w1, w2, gate, back, offs, ka, kb, out_0, out_1, out_2
):
    nc = tc.nc

    with ExitStack() as ctx:
        keep = ctx.enter_context(tc.tile_pool(name="keep", bufs=1))
        shared = ctx.enter_context(tc.tile_pool(name="shared", bufs=1))
        after_table0 = ctx.enter_context(tc.tile_pool(name="after_table0", bufs=1))
        after_h1 = ctx.enter_context(tc.tile_pool(name="after_h1", bufs=1))
        after_w1 = ctx.enter_context(tc.tile_pool(name="after_w1", bufs=1))
        psum = ctx.enter_context(tc.psum_pool(name="psum", bufs=1))

        def entries(list_tile, start, count):
            return list_tile[:, start // LIST_ROWS : (start + count) // LIST_ROWS]

        def quantize(codes, planes, grouped):
            nc.vector.quantize_mx(out=codes.bitcast(FP8X4), scales=planes, in_=grouped)

        offs_sb = keep.tile([P, S // LIST_ROWS], U16, name="offs_sb")
        ka_sb = keep.tile([P, V // LIST_ROWS], U16, name="ka_sb")
        kb_sb = keep.tile([P, V // LIST_ROWS], U16, name="kb_sb")
        table = [after_table0.tile([P, T], U32, name="table0", offset=0, align_bytes=64)]
        table_scales = shared.tile([P, T], U8, name="table_scales", offset=0, align_bytes=64)
        w1_first = after_w1.tile([P, PACK, H], F32, name="w1_raw0", offset=0, align_bytes=64)

        def load_table(o):
            words = x_words[o].rearrange("p n t -> p (n t)").bitcast(I32)
            nc.sync.dma_start(out=table[o][:].bitcast(I32), in_=words)

        nc.gpsimd.memset(table_scales[:, : T // 2].bitcast(I32), 0)
        nc.vector.memset(table_scales[:, T // 2 :].bitcast(I32), 0)
        w1_rows = w1.rearrange("(o p j) c -> o p j c", o=PASSES, j=PACK)
        nc.sync.dma_start(out=w1_first[:, 0, :], in_=w1_rows[0][:, 0, :])
        nc.sync.dma_start(offs_sb[:], offs)
        nc.sync.dma_start(kb_sb[:], kb)
        nc.sync.dma_start(ka_sb[:], ka)
        nc.sync.dma_start(out=w1_first[:, 1, :], in_=w1_rows[0][:, 1, :])
        nc.sync.dma_start(
            out=table_scales[0:P:4, :].bitcast(I32), in_=x_scales.rearrange("o r c -> (o r) c").bitcast(I32)
        )
        nc.sync.dma_start(out=w1_first[:, 2:, :], in_=w1_rows[0][:, 2:, :])
        load_table(0)

        picked_scales = keep.tile([P, S], U8, name="picked_scales", align_bytes=64)
        x_planes = [keep.tile([P, S], U8, name="x_planes0", align_bytes=64)]
        nc.vector.memset(x_planes[0][:].bitcast(I32), 0)
        nc.vector.tensor_copy(picked_scales[:], table_scales[:].indirect(offs_sb[:]))
        x_codes = [keep.tile([P, S], U32, name="x_codes0", align_bytes=64)]
        nc.vector.tensor_copy(x_codes[0][:], table[0][:].indirect(offs_sb[:]))

        def place_scales(o, queue):
            for q in range(QUADRANTS):
                source = 64 * o + 16 * q
                queue.dma_start(
                    out=x_planes[o][32 * q + 4 * o : 32 * q + 4 * o + 4, :].bitcast(I32),
                    in_=picked_scales[source : source + 16 : 4, :].bitcast(I32),
                )

        place_scales(0, nc.sync)
        table.append(shared.tile([P, T], U32, name="table1", offset=0, align_bytes=64))
        load_table(1)

        w1_last = [
            after_table0.tile([P, PACK, H // 2], F32, name="w1_last%d" % n, offset=4096 * n, align_bytes=64) for n in range(2)
        ]
        gate_offset = (8192, 8192 + 4 * EARLY)
        gate_sb = [
            after_table0.tile([P, EARLY], F32, name="gate0", offset=gate_offset[0], align_bytes=64),
            after_table0.tile([P, LATE], F32, name="gate1", offset=gate_offset[1], align_bytes=64),
        ]
        late_back = after_table0.tile([P, LATE], F32, name="late_back", offset=13312, align_bytes=64)
        w2_raw = after_table0.tile([P, PACK, N], F32, name="w2_raw", offset=15360, align_bytes=64)
        for n in range(2):
            nc.sync.dma_start(out=w1_last[n][:], in_=w1_rows[1][:, :, n * H // 2 : (n + 1) * H // 2])
        for c, (start, count) in enumerate(SPANS):
            nc.sync.dma_start(out=gate_sb[c][:], in_=gate[:, start : start + count])
        w2_rows = w2.rearrange("(g j r) c -> j g r c", j=PACK, r=RUN)
        for j in range(PACK):
            nc.sync.dma_start(out=w2_raw[:, j, :], in_=w2_rows[j])
        nc.sync.dma_start(out=late_back[:], in_=back[:, EARLY:])

        w1_grouped = {}
        w1_codes = {}
        w1_planes = {}
        h = {}
        halves = S // BANK
        acc = {}

        def group_w1(grouped, raw, t, copy):
            copy(
                grouped.rearrange("p (g a i) j -> p g a j i", a=RUN // LINE, i=LINE),
                raw.rearrange("p j (g t a i) -> p t g a j i", t=PACK, a=RUN // LINE, i=LINE)[:, t],
            )

        def quantize_w1(o, t):
            n = PACK * o + t
            w1_codes[o, t] = keep.tile([P, P], U32, name="w1_codes%d" % n, align_bytes=64)
            w1_planes[o, t] = keep.tile([P, P], U8, name="w1_planes%d" % n, align_bytes=64)
            quantize(w1_codes[o, t][:], w1_planes[o, t][:], w1_grouped[o, t][:].rearrange("p m j -> p (m j)"))

        def first_product(o, t):
            for half in range(halves):
                tokens = slice(BANK * half, BANK * (half + 1))
                if o == 0:
                    acc[t, half] = psum.tile([P, BANK], F32, name="acc", tag="bank%d" % (halves * t + half))
                nc.tensor.matmul_mx(
                    out=acc[t, half][:],
                    lhsT=w1_codes[o, t][:].bitcast(FP8X4),
                    lhsT_scale=w1_planes[o, t][:],
                    rhs=x_codes[o][:, tokens].bitcast(FP8X4),
                    rhs_scale=x_planes[o][4 * o :, tokens],
                    start=(o == 0),
                    stop=(o == PASSES - 1),
                )

        def relu(t, half, on_vector):
            tokens = slice(BANK * half, BANK * (half + 1))
            if half == 0:
                h[t] = after_h1.tile([P, S], F32, name="h1", offset=0) if t == 1 else keep.tile([P, S], F32, name="h%d" % t)
            if on_vector and t == RELU_ON_VECTOR[-1]:
                cut = BANK * half + BANK // 2
                nc.vector.tensor_scalar(h[t][:, tokens.start : cut], acc[t, half][:, : BANK // 2], 0.0, None, MAX)
                nc.scalar.activation(h[t][:, cut : tokens.stop], acc[t, half][:, BANK // 2 :], RELU)
            elif on_vector:
                nc.vector.tensor_scalar(h[t][:, tokens], acc[t, half][:], 0.0, None, MAX)
            else:
                nc.scalar.activation(h[t][:, tokens], acc[t, half][:], RELU)

        for t in range(PACK):
            w1_grouped[0, t] = keep.tile([P, P, PACK], BF16, name="w1_grouped0_%d" % t, align_bytes=64)
            group_w1(w1_grouped[0, t][:], w1_first[:], t, nc.scalar.copy)
            quantize_w1(0, t)
        x_planes.append(after_w1.tile([P, S], U8, name="x_planes1", offset=0, align_bytes=64))
        nc.vector.memset(x_planes[1][:].bitcast(I32), 0)
        place_scales(1, nc.scalar)
        for t in range(PACK):
            first_product(0, t)
        x_codes.append(keep.tile([P, S], U32, name="x_codes1", align_bytes=64))
        nc.vector.tensor_copy(x_codes[1][:], table[1][:].indirect(offs_sb[:]))
        for t in range(PACK):
            w1_grouped[1, t] = keep.tile([P, P, PACK], BF16, name="w1_grouped1_%d" % t, align_bytes=64)
            group_w1(w1_grouped[1, t][:, : P // 2, :], w1_last[0][:], t, nc.scalar.copy)
        for t in range(PACK):
            group_w1(w1_grouped[1, t][:, P // 2 :, :], w1_last[1][:], t, nc.vector.tensor_copy if t == 0 else nc.scalar.copy)
        for t in range(PACK):
            quantize_w1(1, t)
            first_product(1, t)

        first = [keep.tile([P, PACK, EARLY], F32, name="first0", align_bytes=64)]
        seconds = keep.tile([P, PACK * LATE], F32, name="seconds", align_bytes=64)
        early_start = 2 * LATE - 64
        second = [
            seconds[:, early_start : early_start + PACK * EARLY].rearrange("p (t v) -> p t v", t=PACK),
            seconds[:].rearrange("p (t v) -> p t v", t=PACK),
        ]

        def pick_first(c, t):
            nc.scalar.activation(first[c][:, t, :], h[t][:].indirect(entries(ka_sb, *SPANS[c])), COPY)

        def pick_second(c, t, cols=None):
            cols = cols or slice(0, SPANS[c][1])
            picked = h[t][:].indirect(entries(kb_sb, SPANS[c][0] + cols.start, cols.stop - cols.start))
            nc.vector.tensor_tensor(second[c][:, t, cols], picked, gate_sb[c][:, cols], MULT)

        w2_grouped = keep.tile([P, PACK, P, PACK], BF16, name="w2_grouped", align_bytes=64)
        w2_codes = keep.tile([P, PACK, P], U32, name="w2_codes", align_bytes=64)
        w2_planes = keep.tile([P, PACK, P], U8, name="w2_planes", align_bytes=64)

        for t in range(PACK):
            relu(t, 0, False)
            relu(t, 1, t in RELU_ON_VECTOR)
            if t == RELU_ON_VECTOR[-1]:
                nc.vector.tensor_copy(
                    w2_grouped[:].rearrange("p t m j -> p m j t"), w2_raw[:].rearrange("p j (m t) -> p m j t", t=PACK)
                )
        for t in range(PACK):
            pick_first(0, t)
        for t in range(PACK - 1):
            pick_second(0, t)
        quantize(
            w2_codes[:].rearrange("p t m -> p (t m)"),
            w2_planes[:].rearrange("p t m -> p (t m)"),
            w2_grouped[:].rearrange("p t m j -> p (t m j)"),
        )
        pick_second(0, PACK - 1)
        pick_second(1, 0)
        z_grouped = {}
        z_codes = {}
        z_planes = {}
        y = {}

        def merge(c):
            z_grouped[c] = keep.tile([P, SPANS[c][1], PACK], BF16, name="z_grouped", align_bytes=64)
            for cols in Z_PIECES[c]:
                nc.vector.tensor_tensor(
                    z_grouped[c][:, cols, :].rearrange("p (a i) t -> p a t i", i=LINE),
                    first[c][:, :, cols].rearrange("p t (a i) -> p a t i", i=LINE),
                    second[c][:, :, cols].rearrange("p t (a i) -> p a t i", i=LINE),
                    ADD,
                )

        def quantize_z(c):
            z_codes[c] = keep.tile([P, SPANS[c][1]], U32, name="z_codes%d" % c, align_bytes=64)
            z_planes[c] = keep.tile([P, SPANS[c][1]], U8, name="z_planes%d" % c, align_bytes=64)
            for cols in Z_PIECES[c]:
                quantize(z_codes[c][:, cols], z_planes[c][:, cols], z_grouped[c][:, cols, :].rearrange("p v t -> p (v t)"))

        def second_product(target, c, t, cols):
            nc.tensor.matmul_mx(
                out=target,
                lhsT=w2_codes[:, t, :].bitcast(FP8X4),
                lhsT_scale=w2_planes[:, t, :],
                rhs=z_codes[c][:, cols].bitcast(FP8X4),
                rhs_scale=z_planes[c][:, cols],
                start=True,
                stop=True,
            )

        merge(0)
        quantize_z(0)
        for t in range(1, PACK - 1):
            pick_second(1, t)
        for cols in Z_PIECES[1]:
            pick_second(1, PACK - 1, cols)
        early_bank = psum.tile([P, PACK, EARLY], F32, name="early_bank", tag="bank0")
        for t in range(PACK):
            second_product(early_bank[:, t, :], 0, t, slice(0, EARLY))
        first_offset = gate_offset[1] - 4 * PACK * LATE
        first.append(after_table0.tile([P, PACK, LATE], F32, name="first1", offset=first_offset, align_bytes=64))
        for t in range(PACK - 1):
            pick_first(1, t)
        early_back_sb = after_h1.tile([P, EARLY], F32, name="early_back", offset=0)
        early_back = early_back_sb[:]
        nc.sync.dma_start(out=early_back, in_=back[:, :EARLY])
        early_y = keep.tile([P, PACK, EARLY], F32, name="early_y", align_bytes=64)
        nc.scalar.copy(early_y[:], early_bank[:])
        wide, narrow = Z_PIECES[1]
        last_hidden = h[PACK - 1][:]
        nc.scalar.activation(first[1][:, PACK - 1, wide], last_hidden.indirect(entries(ka_sb, EARLY, wide.stop)), COPY)
        nc.vector.tensor_copy(
            first[1][:, PACK - 1, narrow], last_hidden.indirect(entries(ka_sb, EARLY + narrow.start, LATE - narrow.start))
        )
        for t in range(PACK):
            y[0, t] = early_y[:, t, :]
        merge(1)
        quantize_z(1)
        late_order = (0, 1, 3, 2)
        vector_order = late_order[-1:] + late_order[:-1]
        for t in vector_order:
            late_bank = psum.tile([P, LATE], F32, name="late_bank", tag="bank%d" % (1 + t))
            for cols in (slice(0, 256), slice(256, LATE)):
                second_product(late_bank[:, cols], 1, t, cols)
            late_y = keep.tile([P, LATE], F32, name="late_y%d" % t, align_bytes=64)
            nc.scalar.copy(late_y[:], late_bank[:])
            y[1, t] = late_y[:]
        y_back = {}
        for t in (1, 0, 3, 2):
            y_back[t] = keep.tile([P, LATE], F32, name="y_back%d" % t, align_bytes=64)
            nc.gpsimd.tensor_tensor(y_back[t][:], y[1, t], late_back[:], MULT)

        window = [keep.tile([P, S], F32, name="window%d" % t) for t in range(PACK)]
        out_rows = out_0.rearrange("(p t) c -> p t c", t=PACK)
        shares = ((0, SPLIT), (SPLIT, S))
        pairs = [keep.tile([P, 2, stop - start, 2], BF16, name="pairs%d" % start, align_bytes=64) for start, stop in shares]
        out_grouped = [keep.tile([P, stop - start, PACK], BF16, name="out_grouped%d" % start, align_bytes=64) for start, stop in PIECES]

        def scatter_first(c, t):
            nc.scalar.activation(window[t][:].indirect(entries(ka_sb, *SPANS[c])), y[c, t], COPY)

        def scatter_second(c, t):
            nc.vector.tensor_tensor(window[t][:].indirect(entries(kb_sb, *SPANS[c])), y[c, t], (early_back, late_back[:])[c], MULT)

        for t in range(PACK):
            scatter_first(0, t)
        for t in range(PACK):
            scatter_second(0, t)
        last_tiles = (2, 3)
        for scalar_tile, vector_tile in zip(late_order, vector_order):
            sides = ((ka_sb, y[1, scalar_tile]), (kb_sb, y_back[scalar_tile][:]))
            list_tile, values = sides[scalar_tile != 0]
            nc.scalar.activation(window[scalar_tile][:].indirect(entries(list_tile, *SPANS[1])), values, COPY)
            sides = ((ka_sb, y[1, vector_tile]), (kb_sb, y_back[vector_tile][:]))
            list_tile, values = sides[vector_tile == 0]
            nc.vector.tensor_copy(window[vector_tile][:].indirect(entries(list_tile, *SPANS[1])), values)
            if vector_tile not in last_tiles:
                nc.sync.dma_start(out=out_rows[:, vector_tile, :], in_=window[vector_tile][:])
                for n, (start, stop) in enumerate(shares):
                    nc.gpsimd.tensor_scalar(pairs[n][:, 0, :, vector_tile], window[vector_tile][:, start:stop], 1.0, 1.0, MULT, MULT)
        for t in last_tiles:
            nc.sync.dma_start(out=out_rows[:, t, :], in_=window[t][:])

        out_codes = keep.tile([P, S], U32, name="out_codes", align_bytes=64)
        out_planes = keep.tile([P, S], U8, name="out_planes", align_bytes=64)
        words_out = out_1[0].rearrange("p n t -> p (n t)").bitcast(I32)
        def round_pairs(n, start, stop, copy):
            first_col = shares[n][0]
            for t in last_tiles:
                copy(pairs[n][:, 1, start - first_col : stop - first_col, t - 2], window[t][:, start:stop])

        def weave(n, start, stop, copy, dtype):
            piece = max(k for k in range(len(PIECES)) if PIECES[k][0] <= start)
            count = stop - start
            target = out_grouped[piece][:].rearrange("p c t -> p (c t)").bitcast(dtype).rearrange("p (c u) -> p c u", u=2)
            source = pairs[n][:].rearrange("p u c e -> p u (c e)").bitcast(dtype).rearrange("p u c -> p c u")
            at, first_col = start - PIECES[piece][0], start - shares[n][0]
            copy(target[:, at : at + count, :], source[:, first_col : first_col + count, :])

        round_pairs(0, 0, 256, nc.vector.tensor_copy)
        round_pairs(0, 256, SPLIT, nc.vector.tensor_copy)
        round_pairs(1, SPLIT, LAST_PIECE, nc.scalar.copy)
        round_pairs(1, LAST_PIECE, S, nc.scalar.copy)
        for start, stop in ((0, 256), (256, 512), (512, SPLIT)):
            weave(0, start, stop, nc.vector.tensor_copy, I32)
        for start, stop in ((SPLIT, LAST_PIECE), (LAST_PIECE, S)):
            weave(1, start, stop, nc.scalar.copy, U32)
        for piece, (start, stop) in enumerate(PIECES):
            cols = slice(start, stop)
            quantize(out_codes[:, cols], out_planes[:, cols], out_grouped[piece][:].rearrange("p c t -> p (c t)"))
            if start > 0:
                stored = slice(0 if start == PIECES[1][0] else start, stop)
                nc.sync.dma_start(out=words_out[:, stored], in_=out_codes[:, stored].bitcast(I32))
        for q in range(QUADRANTS):
            queue = nc.scalar if q % 2 else nc.sync
            queue.dma_start(
                out=out_2[0, 4 * q : 4 * q + 4, :].bitcast(I32),
                in_=out_planes[32 * q : 32 * q + 4, :].bitcast(I32),
            )
